import numpy as np
import ml_dtypes


def mxq(x, axis, fmt="e4m3"):
    dtype, down = {"e4m3": (ml_dtypes.float8_e4m3fn, 7), "e5m2": (ml_dtypes.float8_e5m2, 14)}[fmt]
    v = np.moveaxis(np.asarray(x, np.float32).astype(ml_dtypes.bfloat16).astype(np.float64), axis, -1)
    blocks = v.reshape(v.shape[:-1] + (-1, 32))
    amax = np.abs(blocks).max(-1, keepdims=True)
    byte = np.maximum(np.where(amax > 0, np.frexp(amax)[1] - 1 + 127, 0) - down, 1)
    scale = np.exp2(byte - 127.0)
    codes = (blocks / scale).astype(np.float32).astype(dtype).astype(np.float64)
    return np.moveaxis((codes * scale).reshape(v.shape), -1, axis)


WIDE = False


def mx_kscale(k):
    if not WIDE:
        return np.ones(k)
    levels = np.array([10, -10, 5, -5, 0])
    if k % 512:
        return np.exp2(np.random.permutation(np.resize(levels, k // 32))).repeat(32)
    a = np.empty((k // 512, 16))
    for p in range(k // 512):
        a[p, :8] = np.random.permutation(np.resize(levels, 8))
        for g in range(8):
            far = levels[np.abs(levels - a[p, g]) >= 10]
            a[p, g + 8] = far[np.random.randint(len(far))]
    return np.exp2(a.ravel()).repeat(32)


def f64(x):
    return np.asarray(x).astype(np.float64)


def striped(idx):
    return np.tile(idx.reshape(-1, 16).T, (8, 1)).astype(np.uint16)


def unstriped(offs):
    return offs[:16].T.reshape(-1).astype(np.int64)


def sigmoid(v):
    return 1.0 / (1.0 + np.exp(-np.maximum(v, -700.0)))


K, T, E, C, H, N = 512, 512, 8, 256, 512, 384
TOP = 4


def by_expert(wq, xq):
    return np.concatenate([wq[e].T @ xq[:, e * C:(e + 1) * C] for e in range(E)], axis=1)


def setup_inputs():
    n = np.random.standard_normal
    s = mx_kscale(K)[:, None]
    u = mx_kscale(H)
    deal = np.repeat(np.arange(E), C).reshape(TOP, T)[:, np.random.permutation(T)]
    deal = np.take_along_axis(deal, np.argsort(np.random.rand(TOP, T), axis=0), axis=0)
    for _ in range(8):
        s_, t_ = np.random.permutation(T).reshape(2, -1); r = np.random.randint(TOP, size=T // 2); x, y = deal[r, s_].copy(), deal[r, t_].copy()
        ok = ~((deal[:, s_] == y).any(0) | (deal[:, t_] == x).any(0)); deal[r[ok], s_[ok]] = y[ok]; deal[r[ok], t_[ok]] = x[ok]
    order = np.lexsort((np.random.rand(TOP * T), deal.reshape(-1)))
    slot_token = order % T; pos = np.empty(TOP * T, np.int64); pos[order] = np.arange(TOP * T); pos = pos.reshape(TOP, T)
    g = np.random.uniform(0.5, 1.5, (TOP, T)); g = g / g.sum(0)
    return {
        "xT": (n((K, T)) * s).astype(np.float32),
        "w1": (n((E, K, H)) / np.sqrt(K) / s[None]).astype(np.float32),
        "w3": (n((E, K, H)) / np.sqrt(K) / s[None] * u[None, None, :]).astype(np.float32),
        "w2": (n((E, H, N)) / np.sqrt(H) / u[None, :, None]).astype(np.float32),
        "gate": np.stack([np.tile(r, (N, 1)) for r in g]).astype(np.float32),
        "offs": striped(slot_token),
        "pos1": striped(pos[0]),
        "pos2": striped(pos[1]),
        "pos3": striped(pos[2]),
        "pos4": striped(pos[3]),
    }


def reference(xT, w1, w3, w2, gate, offs, pos1, pos2, pos3, pos4):
    idx = unstriped(offs)
    xq = mxq(f64(xT)[:, idx], 0, "e4m3")
    h = sigmoid(by_expert(mxq(f64(w1), 1, "e4m3"), xq))
    h = h * by_expert(mxq(f64(w3), 1, "e4m3"), xq)
    y = by_expert(mxq(f64(w2), 1, "e4m3"), mxq(h, 0, "e4m3"))
    return sum(f64(gate[r]) * y[:, unstriped(p)] for r, p in enumerate((pos1, pos2, pos3, pos4)))

@@ -1,0 +1,247 @@
+from contextlib import ExitStack
+
+import concourse.mybir as mybir
+
+E, C, T, K, H, N, R = 8, 256, 512, 512, 512, 384, 4
+S = E * C
+FLOPS = 2 * S * (2 * K * H + H * N)
+
+F32 = mybir.dt.float32
+BF16 = mybir.dt.bfloat16
+U32 = mybir.dt.uint32
+U16 = mybir.dt.uint16
+U8 = mybir.dt.uint8
+FP8X4 = mybir.dt.float8_e4m3fn_x4
+SIGMOID = mybir.ActivationFunctionType.Sigmoid
+COPY = mybir.ActivationFunctionType.Copy
+MULT = mybir.AluOpType.mult
+ADD = mybir.AluOpType.add
+
+P = 128
+PACK = 4
+NCHUNKS = N // P
+RAW_BUFS = 12
+
+
+def tile_moe_tk_glu_sigmoid_kernel(
+    tc, xT, w1, w3, w2, gate, offs, pos1, pos2, pos3, pos4, out
+):
+    nc = tc.nc
+    with ExitStack() as ctx:
+        held = ctx.enter_context(tc.tile_pool(name="held", bufs=1))
+        rawp = ctx.enter_context(tc.tile_pool(name="rawp", bufs=RAW_BUFS))
+        grp = ctx.enter_context(tc.tile_pool(name="grp", bufs=6))
+        codep = ctx.enter_context(tc.tile_pool(name="codep", bufs=6))
+        prodp = ctx.enter_context(tc.tile_pool(name="prodp", bufs=2))
+        work = ctx.enter_context(tc.tile_pool(name="work", bufs=2))
+        psa = ctx.enter_context(tc.psum_pool(name="psa", bufs=3))
+        psg = ctx.enter_context(tc.psum_pool(name="psg", bufs=3))
+        psy = ctx.enter_context(tc.psum_pool(name="psy", bufs=2))
+
+        warm = held.tile([P, 1], F32, name="warm")
+        warm_out = held.tile([P, 1], F32, name="warm_out")
+        nc.gpsimd.memset(warm[:], 0.0)
+        nc.scalar.activation(warm_out[:], warm[:], SIGMOID)
+
+        x_codes = held.tile([P, T], U32, name="x_codes", align_bytes=64)
+        x_scales = held.tile([P, T], U8, name="x_scales", align_bytes=64)
+        nc.gpsimd.memset(x_scales[:], 0)
+
+        x_raw = held.tile([P, PACK, T], F32, name="x_raw")
+        nc.sync.dma_start(out=x_raw[:], in_=xT.rearrange("(p j) t -> p j t", j=PACK))
+        offs_t = held.tile([P, S // 16], U16, name="offs_t")
+        nc.sync.dma_start(offs_t[:], offs)
+
+        raws = {}
+        loads = []
+        for e in range(E):
+            loads += [("w1", e, 0), ("w3", e, 0)]
+        loads += [("w2", 0, 0), ("w2", 0, 1), ("w2", 1, 0), ("w2", 1, 1), ("gate", 0, 0)]
+        loads += [("w2", 2, 0), ("w2", 2, 1), ("gate", 1, 0), ("gate", 2, 0)]
+
+        def load_next():
+            if not loads:
+                return
+            kind, i, hh = loads.pop(0)
+            raw = rawp.tile([P, 4, T], F32, name="raw")
+            if kind == "w1":
+                nc.sync.dma_start(out=raw[:], in_=w1[i, :, :].rearrange("(p j) h -> p j h", j=PACK))
+            elif kind == "w3":
+                nc.sync.dma_start(out=raw[:], in_=w3[i, :, :].rearrange("(p j) h -> p j h", j=PACK))
+            elif kind == "w2":
+                for q in range(4):
+                    nc.sync.dma_start(
+                        out=raw[:, q, :].rearrange("p (j n) -> p j n", j=PACK),
+                        in_=w2[4 * hh + q, :, i * P : (i + 1) * P].rearrange("(p j) n -> p j n", j=PACK),
+                    )
+            else:
+                nc.sync.dma_start(
+                    out=raw[:], in_=gate[:, i * P : (i + 1) * P, :].rearrange("r n t -> n r t")
+                )
+            raws[kind, i, hh] = raw
+
+        for q in range(RAW_BUFS):
+            load_next()
+
+        pos_t = []
+        for r, pos in enumerate((pos1, pos2, pos3, pos4)):
+            pt = held.tile([P, T // 16], U16, name=f"pos_t{r}")
+            nc.sync.dma_start(pt[:], pos)
+            pos_t.append(pt)
+
+        def plain_copy(on_vector, dst, src):
+            src = src.rearrange("p j (c i) -> p c j i", i=4)
+            dst = dst.rearrange("p (c i j) -> p c j i", i=4, j=PACK)
+            if on_vector:
+                nc.vector.tensor_copy(out=dst, in_=src)
+            else:
+                nc.scalar.activation(dst, src, COPY)
+
+        x_grouped = held.tile([P, T * PACK], BF16, name="x_grouped", align_bytes=64)
+        plain_copy(True, x_grouped[:], x_raw[:])
+        nc.vector.quantize_mx(out=x_codes[:].bitcast(FP8X4), scales=x_scales[:], in_=x_grouped[:])
+
+        y_rows = []
+        for c in range(NCHUNKS):
+            yt = held.tile([P, S], F32, name=f"y_rows{c}")
+            y_rows.append(yt)
+        weights, gathered, h_codes, w2_codes = {}, {}, {}, {}
+        y_done = []
+
+        def quantize(grouped):
+            codes = codep.tile([P, H], U32, name="codes", align_bytes=64)
+            scales = codep.tile([P, H], U8, name="scales", align_bytes=64)
+            nc.vector.quantize_mx(out=codes[:].bitcast(FP8X4), scales=scales[:], in_=grouped[:])
+            return codes, scales
+
+        def gather(e):
+            cols = slice(e * (C // 16), (e + 1) * (C // 16))
+            g_codes = held.tile([P, C], U32, name=f"g_codes{e}", align_bytes=64)
+            g_scales = held.tile([P, C], U8, name=f"g_scales{e}", align_bytes=64)
+            nc.vector.tensor_copy(g_codes[:], x_codes[:].indirect(offs_t[:, cols]))
+            nc.vector.tensor_copy(g_scales[:], x_scales[:].indirect(offs_t[:, cols]))
+            gathered[e] = (g_codes, g_scales)
+
+        def prepare(kind, e, vector_halves):
+            raw = raws[kind, e, 0]
+            grouped = grp.tile([P, H * PACK], BF16, name="grouped", align_bytes=64)
+            src = raw[:].rearrange("p j (m t) -> p m j t", t=4)
+            dst = grouped[:].rearrange("p (t m j) -> p m j t", t=4, j=PACK)
+            if len(vector_halves) == 2:
+                nc.vector.tensor_copy(out=dst, in_=src)
+            elif not vector_halves:
+                nc.scalar.copy(out=dst, in_=src)
+            else:
+                for half in range(2):
+                    d, s = dst[:, :, :, 2 * half : 2 * half + 2], src[:, :, :, 2 * half : 2 * half + 2]
+                    if half in vector_halves:
+                        nc.vector.tensor_copy(out=d, in_=s)
+                    else:
+                        nc.scalar.copy(out=d, in_=s)
+            weights[kind, e] = quantize(grouped)
+
+        def prepare_w2(c, hh, on_vector):
+            raw = raws["w2", c, hh]
+            grouped = grp.tile([P, H * PACK], BF16, name="grouped", align_bytes=64)
+            for q in range(4):
+                plain_copy(
+                    q < on_vector,
+                    grouped[:, q * 512 : (q + 1) * 512],
+                    raw[:, q, :].rearrange("p (j n) -> p j n", j=PACK),
+                )
+            w2_codes[c, hh] = quantize(grouped)
+
+        def first_layer(e):
+            g_codes, g_scales = gathered.pop(e)
+            host = raws["w1", min(e + 1, E - 1), 0]
+            h_grouped = work.tile([P, C, PACK], BF16, name="h_grouped", align_bytes=64)
+            for s in range(C // P):
+                slots = slice(s * P, (s + 1) * P)
+                accs = []
+                for kind, pool in (("w1", psa), ("w3", psg)):
+                    acc = pool.tile([P, PACK, P], F32, name=f"acc_{kind}")
+                    codes, scales = weights[kind, e]
+                    for t in range(PACK):
+                        nc.tensor.matmul_mx(
+                            out=acc[:, t, :],
+                            lhsT=codes[:, t * P : (t + 1) * P].bitcast(FP8X4),
+                            lhsT_scale=scales[:, t * P : (t + 1) * P],
+                            rhs=g_codes[:, slots].bitcast(FP8X4),
+                            rhs_scale=g_scales[:, slots],
+                            start=True,
+                            stop=True,
+                        )
+                    accs.append(acc[:].rearrange("p t s -> p s t"))
+                sig = host[:, s + (2 if e == E - 1 else 0), :].rearrange("p (s t) -> p s t", t=PACK)
+                nc.scalar.activation(sig, accs[0], SIGMOID)
+                nc.vector.tensor_tensor(h_grouped[:, slots, :], sig, accs[1], MULT)
+            hc = held.tile([P, C], U32, name=f"h_codes{e}", align_bytes=64)
+            hs = held.tile([P, C], U8, name=f"h_scales{e}", align_bytes=64)
+            nc.vector.quantize_mx(
+                out=hc[:].bitcast(FP8X4), scales=hs[:], in_=h_grouped[:].rearrange("p s t -> p (s t)")
+            )
+            h_codes[e] = (hc, hs)
+
+        def second_layer():
+            for c in range(NCHUNKS):
+                for pair in range(E // 2):
+                    if (c, pair) in y_done or (c, pair // 2) not in w2_codes or 2 * pair + 1 not in h_codes:
+                        continue
+                    y_done.append((c, pair))
+                    codes, scales = w2_codes[c, pair // 2]
+                    acc = psy.tile([P, 2 * C], F32, name="acc_y")
+                    for q in range(2):
+                        e = 2 * pair + q
+                        wcols = slice((e % 4) * P, (e % 4 + 1) * P)
+                        hc, hs = h_codes[e]
+                        nc.tensor.matmul_mx(
+                            out=acc[:, q * C : (q + 1) * C],
+                            lhsT=codes[:, wcols].bitcast(FP8X4),
+                            lhsT_scale=scales[:, wcols],
+                            rhs=hc[:].bitcast(FP8X4),
+                            rhs_scale=hs[:],
+                            start=True,
+                            stop=True,
+                        )
+                    nc.scalar.copy(out=y_rows[c][:, 2 * pair * C : 2 * (pair + 1) * C], in_=acc[:])
+
+        def combine(c):
+            gates = raws["gate", c, 0]
+            prods = prodp.tile([P, R, T], F32, name="prods")
+            for r in range(R):
+                nc.vector.tensor_tensor(prods[:, r, :], y_rows[c][:].indirect(pos_t[r][:]), gates[:, r, :], MULT)
+            rows = out[c * P : (c + 1) * P, :]
+            if c < NCHUNKS - 1:
+                nc.vector.tensor_tensor(prods[:, 0:2, :], prods[:, 0:2, :], prods[:, 2:4, :], ADD)
+                nc.vector.tensor_tensor(prods[:, 0, :], prods[:, 0, :], prods[:, 1, :], ADD)
+                nc.sync.dma_start(out=rows, in_=prods[:, 0, :])
+            else:
+                nc.vector.tensor_tensor(prods[:, 0, :], prods[:, 0, :], prods[:, 1, :], ADD)
+                nc.vector.tensor_tensor(prods[:, 2, :], prods[:, 2, :], prods[:, 3, :], ADD)
+                for half in range(2):
+                    cols = slice(half * (T // 2), (half + 1) * (T // 2))
+                    nc.vector.tensor_tensor(prods[:, 0, cols], prods[:, 0, cols], prods[:, 2, cols], ADD)
+                    nc.sync.dma_start(out=rows[:, cols], in_=prods[:, 0, cols])
+
+        for e in range(E):
+            gather(e)
+            prepare("w1", e, (0,) if e in (2, 3) else ())
+            if e == 0:
+                load_next()
+            prepare("w3", e, (0, 1) if e >= 4 else (0,) if e >= 2 else ())
+            load_next()
+            if e > 0:
+                first_layer(e - 1)
+                load_next()
+        first_layer(E - 1)
+        load_next()
+
+        V2 = {(0, 0): 2, (0, 1): 1, (1, 0): 4, (1, 1): 4, (2, 1): 1}
+        for c in range(NCHUNKS):
+            for hh in range(2):
+                prepare_w2(c, hh, V2.get((c, hh), 0))
+                load_next()
+                second_layer()
+            if c > 0:
+                combine(c - 1)
+        combine(NCHUNKS - 1)

@@ -1,6 +1,7 @@
 from contextlib import ExitStack
 
 import concourse.mybir as mybir
+from concourse.masks import make_identity
 
 E, C, T, K, H, N, R = 8, 256, 512, 512, 512, 384, 4
 S = E * C
@@ -20,7 +21,7 @@ ADD = mybir.AluOpType.add
 P = 128
 PACK = 4
 NCHUNKS = N // P
-RAW_BUFS = 12
+RAW_BUFS = 11
 
 
 def tile_moe_tk_glu_sigmoid_kernel(
@@ -30,9 +31,9 @@ def tile_moe_tk_glu_sigmoid_kernel(
     with ExitStack() as ctx:
         held = ctx.enter_context(tc.tile_pool(name="held", bufs=1))
         rawp = ctx.enter_context(tc.tile_pool(name="rawp", bufs=RAW_BUFS))
-        grp = ctx.enter_context(tc.tile_pool(name="grp", bufs=6))
-        codep = ctx.enter_context(tc.tile_pool(name="codep", bufs=6))
-        prodp = ctx.enter_context(tc.tile_pool(name="prodp", bufs=2))
+        grp = ctx.enter_context(tc.tile_pool(name="grp", bufs=3))
+        codep = ctx.enter_context(tc.tile_pool(name="codep", bufs=3))
+        prodp = ctx.enter_context(tc.tile_pool(name="prodp", bufs=1))
         work = ctx.enter_context(tc.tile_pool(name="work", bufs=2))
         psa = ctx.enter_context(tc.psum_pool(name="psa", bufs=3))
         psg = ctx.enter_context(tc.psum_pool(name="psg", bufs=3))
@@ -42,6 +43,11 @@ def tile_moe_tk_glu_sigmoid_kernel(
         warm_out = held.tile([P, 1], F32, name="warm_out")
         nc.gpsimd.memset(warm[:], 0.0)
         nc.scalar.activation(warm_out[:], warm[:], SIGMOID)
+
+        gate_cols = held.tile([P, R, PACK], F32, name="gate_cols")
+        nc.scalar.dma_start(out=gate_cols[:], in_=gate[:, 0, :].rearrange("r (q c) -> q r c", c=PACK))
+        ident = held.tile([P, P], F32, name="ident")
+        make_identity(nc, ident[:])
 
         x_codes = held.tile([P, T], U32, name="x_codes", align_bytes=64)
         x_scales = held.tile([P, T], U8, name="x_scales", align_bytes=64)
@@ -55,29 +61,29 @@ def tile_moe_tk_glu_sigmoid_kernel(
         raws = {}
         loads = []
         for e in range(E):
-            loads += [("w1", e, 0), ("w3", e, 0)]
-        loads += [("w2", 0, 0), ("w2", 0, 1), ("w2", 1, 0), ("w2", 1, 1), ("gate", 0, 0)]
-        loads += [("w2", 2, 0), ("w2", 2, 1), ("gate", 1, 0), ("gate", 2, 0)]
+            loads += [("w3", e, 0), ("w1", e, 0)]
+            if e == 5:
+                loads += [("w2", 0, 0)]
+        loads += [("w2", 0, 1), ("w2", 1, 0), ("w2", 1, 1), ("w2", 2, 0), ("w2", 2, 1)]
 
         def load_next():
             if not loads:
                 return
             kind, i, hh = loads.pop(0)
-            raw = rawp.tile([P, 4, T], F32, name="raw")
+            if (kind, i, hh) in (("w2", 0, 0), ("w2", 2, 0)):
+                raw = held.tile([P, 4, T], F32, name="raw_apart", tag="apart")
+            else:
+                raw = rawp.tile([P, 4, T], F32, name="raw")
             if kind == "w1":
                 nc.sync.dma_start(out=raw[:], in_=w1[i, :, :].rearrange("(p j) h -> p j h", j=PACK))
             elif kind == "w3":
                 nc.sync.dma_start(out=raw[:], in_=w3[i, :, :].rearrange("(p j) h -> p j h", j=PACK))
-            elif kind == "w2":
+            else:
                 for q in range(4):
                     nc.sync.dma_start(
                         out=raw[:, q, :].rearrange("p (j n) -> p j n", j=PACK),
                         in_=w2[4 * hh + q, :, i * P : (i + 1) * P].rearrange("(p j) n -> p j n", j=PACK),
                     )
-            else:
-                nc.sync.dma_start(
-                    out=raw[:], in_=gate[:, i * P : (i + 1) * P, :].rearrange("r n t -> n r t")
-                )
             raws[kind, i, hh] = raw
 
         for q in range(RAW_BUFS):
@@ -89,6 +95,15 @@ def tile_moe_tk_glu_sigmoid_kernel(
             nc.sync.dma_start(pt[:], pos)
             pos_t.append(pt)
 
+        gates = held.tile([P, R, T], F32, name="gates")
+        for r in range(R):
+            spread = (psa if r % 2 == 0 else psg).tile([P, PACK, P], F32, name="acc_w1" if r % 2 == 0 else "acc_w3")
+            for c in range(PACK):
+                nc.tensor.transpose(spread[:, c, :], gate_cols[:, r, c : c + 1].to_broadcast([P, P]), ident[:])
+            nc.scalar.copy(
+                out=gates[:, r, :].rearrange("p (q c) -> p q c", c=PACK), in_=spread[:].rearrange("p c q -> p q c")
+            )
+
         def plain_copy(on_vector, dst, src):
             src = src.rearrange("p j (c i) -> p c j i", i=4)
             dst = dst.rearrange("p (c i j) -> p c j i", i=4, j=PACK)
@@ -97,7 +112,7 @@ def tile_moe_tk_glu_sigmoid_kernel(
             else:
                 nc.scalar.activation(dst, src, COPY)
 
-        x_grouped = held.tile([P, T * PACK], BF16, name="x_grouped", align_bytes=64)
+        x_grouped = held.tile([P, T * PACK], BF16, name="x_grouped", tag="x_grouped", align_bytes=64)
         plain_copy(True, x_grouped[:], x_raw[:])
         nc.vector.quantize_mx(out=x_codes[:].bitcast(FP8X4), scales=x_scales[:], in_=x_grouped[:])
 
@@ -105,12 +120,12 @@ def tile_moe_tk_glu_sigmoid_kernel(
         for c in range(NCHUNKS):
             yt = held.tile([P, S], F32, name=f"y_rows{c}")
             y_rows.append(yt)
-        weights, gathered, h_codes, w2_codes = {}, {}, {}, {}
+        weights, gathered, h_codes, w2_codes, pairs, hidden = {}, {}, {}, {}, {}, {}
         y_done = []
 
         def quantize(grouped):
-            codes = codep.tile([P, H], U32, name="codes", align_bytes=64)
-            scales = codep.tile([P, H], U8, name="scales", align_bytes=64)
+            codes = codep.tile([P, H], U32, name="w2_codes", align_bytes=64)
+            scales = codep.tile([P, H], U8, name="w2_scales", align_bytes=64)
             nc.vector.quantize_mx(out=codes[:].bitcast(FP8X4), scales=scales[:], in_=grouped[:])
             return codes, scales
 
@@ -122,11 +137,13 @@ def tile_moe_tk_glu_sigmoid_kernel(
             nc.vector.tensor_copy(g_scales[:], x_scales[:].indirect(offs_t[:, cols]))
             gathered[e] = (g_codes, g_scales)
 
-        def prepare(kind, e, vector_halves):
+        def interleave(kind, e, vector_halves):
             raw = raws[kind, e, 0]
-            grouped = grp.tile([P, H * PACK], BF16, name="grouped", align_bytes=64)
+            if kind == "w3":
+                pairs[e] = grp.tile([P, 2, H * PACK], BF16, name="grouped", align_bytes=64)
+            grouped = pairs[e][:, 0 if kind == "w1" else 1, :]
             src = raw[:].rearrange("p j (m t) -> p m j t", t=4)
-            dst = grouped[:].rearrange("p (t m j) -> p m j t", t=4, j=PACK)
+            dst = grouped.rearrange("p (t m j) -> p m j t", t=4, j=PACK)
             if len(vector_halves) == 2:
                 nc.vector.tensor_copy(out=dst, in_=src)
             elif not vector_halves:
@@ -138,14 +155,30 @@ def tile_moe_tk_glu_sigmoid_kernel(
                         nc.vector.tensor_copy(out=d, in_=s)
                     else:
                         nc.scalar.copy(out=d, in_=s)
-            weights[kind, e] = quantize(grouped)
+
+        def quantize_pair(e):
+            codes = codep.tile([P, 2 * H], U32, name="codes", align_bytes=64)
+            scales = codep.tile([P, 2 * H], U8, name="scales", align_bytes=64)
+            if e < E - 1:
+                nc.vector.quantize_mx(
+                    out=codes[:].bitcast(FP8X4), scales=scales[:], in_=pairs[e][:].rearrange("p k c -> p (k c)")
+                )
+            else:
+                for k in (1, 0):
+                    cols = slice(k * H, (k + 1) * H)
+                    nc.vector.quantize_mx(out=codes[:, cols].bitcast(FP8X4), scales=scales[:, cols], in_=pairs[e][:, k, :])
+            weights["w1", e] = (codes[:, 0:H], scales[:, 0:H])
+            weights["w3", e] = (codes[:, H : 2 * H], scales[:, H : 2 * H])
 
         def prepare_w2(c, hh, on_vector):
             raw = raws["w2", c, hh]
-            grouped = grp.tile([P, H * PACK], BF16, name="grouped", align_bytes=64)
+            if hh == 1 and c == 2:
+                grouped = held.tile([P, H * PACK], BF16, name="late_grouped", tag=f"late{c}", align_bytes=64)
+            else:
+                grouped = grp.tile([P, H * PACK], BF16, name="grouped", align_bytes=64)
             for q in range(4):
                 plain_copy(
-                    q < on_vector,
+                    q >= 4 - on_vector,
                     grouped[:, q * 512 : (q + 1) * 512],
                     raw[:, q, :].rearrange("p (j n) -> p j n", j=PACK),
                 )
@@ -153,7 +186,10 @@ def tile_moe_tk_glu_sigmoid_kernel(
 
         def first_layer(e):
             g_codes, g_scales = gathered.pop(e)
-            host = raws["w1", min(e + 1, E - 1), 0]
+            if e == E - 1:
+                host, row = held.tile([P, 2, T], F32, name="last_sig", tag="x_grouped", align_bytes=64), 0
+            else:
+                host, row = (raws["w1", 2, 0], 2 * e) if e < 2 else (raws["w1", e + 1, 0], 0)
             h_grouped = work.tile([P, C, PACK], BF16, name="h_grouped", align_bytes=64)
             for s in range(C // P):
                 slots = slice(s * P, (s + 1) * P)
@@ -172,13 +208,16 @@ def tile_moe_tk_glu_sigmoid_kernel(
                             stop=True,
                         )
                     accs.append(acc[:].rearrange("p t s -> p s t"))
-                sig = host[:, s + (2 if e == E - 1 else 0), :].rearrange("p (s t) -> p s t", t=PACK)
+                sig = host[:, s + row, :].rearrange("p (s t) -> p s t", t=PACK)
                 nc.scalar.activation(sig, accs[0], SIGMOID)
                 nc.vector.tensor_tensor(h_grouped[:, slots, :], sig, accs[1], MULT)
+            hidden[e] = h_grouped
+
+        def quantize_hidden(e):
             hc = held.tile([P, C], U32, name=f"h_codes{e}", align_bytes=64)
             hs = held.tile([P, C], U8, name=f"h_scales{e}", align_bytes=64)
             nc.vector.quantize_mx(
-                out=hc[:].bitcast(FP8X4), scales=hs[:], in_=h_grouped[:].rearrange("p s t -> p (s t)")
+                out=hc[:].bitcast(FP8X4), scales=hs[:], in_=hidden[e][:].rearrange("p s t -> p (s t)")
             )
             h_codes[e] = (hc, hs)
 
@@ -206,42 +245,74 @@ def tile_moe_tk_glu_sigmoid_kernel(
                     nc.scalar.copy(out=y_rows[c][:, 2 * pair * C : 2 * (pair + 1) * C], in_=acc[:])
 
         def combine(c):
-            gates = raws["gate", c, 0]
-            prods = prodp.tile([P, R, T], F32, name="prods")
-            for r in range(R):
-                nc.vector.tensor_tensor(prods[:, r, :], y_rows[c][:].indirect(pos_t[r][:]), gates[:, r, :], MULT)
-            rows = out[c * P : (c + 1) * P, :]
-            if c < NCHUNKS - 1:
-                nc.vector.tensor_tensor(prods[:, 0:2, :], prods[:, 0:2, :], prods[:, 2:4, :], ADD)
-                nc.vector.tensor_tensor(prods[:, 0, :], prods[:, 0, :], prods[:, 1, :], ADD)
-                nc.sync.dma_start(out=rows, in_=prods[:, 0, :])
+            if c == 1:
+                first = held.tile([P, 4, T], F32, name="first", tag="apart")
+                second = held.tile([P, 2, T], F32, name="second", tag="late2", align_bytes=64)
+                prods = [first[:, 0, :], first[:, 1, :], second[:, 0, :], second[:, 1, :]]
             else:
-                nc.vector.tensor_tensor(prods[:, 0, :], prods[:, 0, :], prods[:, 1, :], ADD)
-                nc.vector.tensor_tensor(prods[:, 2, :], prods[:, 2, :], prods[:, 3, :], ADD)
+                whole = prodp.tile([P, R, T], F32, name="prods")
+                prods = [whole[:, r, :] for r in range(R)]
+            for r in range(R):
+                nc.vector.tensor_tensor(prods[r], y_rows[c][:].indirect(pos_t[r][:]), gates[:, r, :], MULT)
+            rows = out[c * P : (c + 1) * P, :]
+            last = c == NCHUNKS - 1
+            terms = 2 if last else R
+            turned = psy.tile([P, 2 * C], F32, name="acc_y")
+            for r in range(terms):
+                for b in range(T // P):
+                    cols = slice(b * P, (b + 1) * P)
+                    nc.tensor.matmul(
+                        turned[:, cols],
+                        lhsT=prods[r][:, cols],
+                        rhs=ident[:],
+                        start=r == 0 and b == 0,
+                        stop=r == terms - 1 and b == T // P - 1,
+                        is_transpose=True,
+                    )
+            turned_sb = work.tile([P, T], F32, name="turned_sb")
+            nc.scalar.copy(out=turned_sb[:], in_=turned[:])
+            back = psa.tile([P, T], F32, name="acc_w1")
+            for b in range(T // P):
+                cols = slice(b * P, (b + 1) * P)
+                nc.tensor.transpose(back[:, cols], turned_sb[:, cols], ident[:])
+            sums = work.tile([P, T], F32, name="sums")
+            if not last:
+                nc.scalar.copy(out=sums[:], in_=back[:])
+                nc.sync.dma_start(out=rows, in_=sums[:])
+            else:
+                nc.vector.tensor_tensor(prods[2], prods[2], prods[3], ADD)
                 for half in range(2):
                     cols = slice(half * (T // 2), (half + 1) * (T // 2))
-                    nc.vector.tensor_tensor(prods[:, 0, cols], prods[:, 0, cols], prods[:, 2, cols], ADD)
-                    nc.sync.dma_start(out=rows[:, cols], in_=prods[:, 0, cols])
+                    nc.vector.tensor_tensor(sums[:, cols], prods[2][:, cols], back[:, cols], ADD)
+                    nc.sync.dma_start(out=rows[:, cols], in_=sums[:, cols])
 
         for e in range(E):
             gather(e)
-            prepare("w1", e, (0,) if e in (2, 3) else ())
-            if e == 0:
-                load_next()
-            prepare("w3", e, (0, 1) if e >= 4 else (0,) if e >= 2 else ())
+        for e in range(E):
+            interleave("w3", e, (0, 1) if e >= 3 else ())
             load_next()
-            if e > 0:
+            interleave("w1", e, (0,) if e == E - 1 else ())
+            load_next()
+            if e == 3:
+                quantize_hidden(0)
+            if e >= 3:
+                quantize_hidden(e - 2)
+            if e == 6:
+                prepare_w2(0, 0, 0)
+            quantize_pair(e)
+            if e == 2:
+                first_layer(0)
+            if e >= 2:
                 first_layer(e - 1)
-                load_next()
+            second_layer()
+        quantize_hidden(E - 2)
         first_layer(E - 1)
-        load_next()
-
-        V2 = {(0, 0): 2, (0, 1): 1, (1, 0): 4, (1, 1): 4, (2, 1): 1}
-        for c in range(NCHUNKS):
+        prepare_w2(0, 1, 0)
+        quantize_hidden(E - 1)
+        second_layer()
+        for c in range(1, NCHUNKS):
             for hh in range(2):
-                prepare_w2(c, hh, V2.get((c, hh), 0))
-                load_next()
+                prepare_w2(c, hh, 4 if (c, hh) == (2, 0) else 0)
                 second_layer()
-            if c > 0:
-                combine(c - 1)
+            combine(c - 1)
         combine(NCHUNKS - 1)

@@ -22,6 +22,8 @@ P = 128
 PACK = 4
 NCHUNKS = N // P
 RAW_BUFS = 11
+GROUP = 4
+WINDOW = 1408
 
 
 def tile_moe_tk_glu_sigmoid_kernel(
@@ -49,11 +51,12 @@ def tile_moe_tk_glu_sigmoid_kernel(
         ident = held.tile([P, P], F32, name="ident")
         make_identity(nc, ident[:])
 
-        x_codes = held.tile([P, T], U32, name="x_codes", align_bytes=64)
-        x_scales = held.tile([P, T], U8, name="x_scales", align_bytes=64)
-        nc.gpsimd.memset(x_scales[:], 0)
+        x_codes = held.tile([P, WINDOW], U32, name="x_codes", align_bytes=64)
+        x_scales = held.tile([P, WINDOW], U8, name="x_scales", align_bytes=64)
+        nc.gpsimd.memset(x_scales[:].bitcast(U32), 0)
+        nc.gpsimd.memset(x_codes[:, T:], 0)
 
-        x_raw = held.tile([P, PACK, T], F32, name="x_raw")
+        x_raw = held.tile([P, PACK, T], F32, name="x_raw", tag="late1", align_bytes=64)
         nc.sync.dma_start(out=x_raw[:], in_=xT.rearrange("(p j) t -> p j t", j=PACK))
         offs_t = held.tile([P, S // 16], U16, name="offs_t")
         nc.sync.dma_start(offs_t[:], offs)
@@ -114,13 +117,13 @@ def tile_moe_tk_glu_sigmoid_kernel(
 
         x_grouped = held.tile([P, T * PACK], BF16, name="x_grouped", tag="x_grouped", align_bytes=64)
         plain_copy(True, x_grouped[:], x_raw[:])
-        nc.vector.quantize_mx(out=x_codes[:].bitcast(FP8X4), scales=x_scales[:], in_=x_grouped[:])
+        nc.vector.quantize_mx(out=x_codes[:, :T].bitcast(FP8X4), scales=x_scales[:, :T], in_=x_grouped[:])
 
         y_rows = []
         for c in range(NCHUNKS):
             yt = held.tile([P, S], F32, name=f"y_rows{c}")
             y_rows.append(yt)
-        weights, gathered, h_codes, w2_codes, pairs, hidden = {}, {}, {}, {}, {}, {}
+        weights, gathered, h_codes, w2_codes, pairs, hidden, products = {}, {}, {}, {}, {}, {}, {}
         y_done = []
 
         def quantize(grouped):
@@ -129,28 +132,29 @@ def tile_moe_tk_glu_sigmoid_kernel(
             nc.vector.quantize_mx(out=codes[:].bitcast(FP8X4), scales=scales[:], in_=grouped[:])
             return codes, scales
 
-        def gather(e):
-            cols = slice(e * (C // 16), (e + 1) * (C // 16))
-            g_codes = held.tile([P, C], U32, name=f"g_codes{e}", align_bytes=64)
-            g_scales = held.tile([P, C], U8, name=f"g_scales{e}", align_bytes=64)
+        def gather(g):
+            cols = slice(g * (GROUP * C // 16), (g + 1) * (GROUP * C // 16))
+            g_codes = held.tile([P, GROUP * C], U32, name=f"g_codes{g}", align_bytes=64)
+            g_scales = held.tile([P, GROUP * C], U8, name=f"g_scales{g}", align_bytes=64)
             nc.vector.tensor_copy(g_codes[:], x_codes[:].indirect(offs_t[:, cols]))
             nc.vector.tensor_copy(g_scales[:], x_scales[:].indirect(offs_t[:, cols]))
-            gathered[e] = (g_codes, g_scales)
+            for q in range(GROUP):
+                gathered[GROUP * g + q] = (g_codes[:, q * C : (q + 1) * C], g_scales[:, q * C : (q + 1) * C])
 
         def interleave(kind, e, vector_halves):
             raw = raws[kind, e, 0]
             if kind == "w3":
                 pairs[e] = grp.tile([P, 2, H * PACK], BF16, name="grouped", align_bytes=64)
             grouped = pairs[e][:, 0 if kind == "w1" else 1, :]
-            src = raw[:].rearrange("p j (m t) -> p m j t", t=4)
-            dst = grouped.rearrange("p (t m j) -> p m j t", t=4, j=PACK)
+            src = raw[:].rearrange("p j (m u v) -> p u m j v", u=2, v=2)
+            dst = grouped.rearrange("p (u v m j) -> p u m j v", u=2, v=2, j=PACK)
             if len(vector_halves) == 2:
                 nc.vector.tensor_copy(out=dst, in_=src)
             elif not vector_halves:
                 nc.scalar.copy(out=dst, in_=src)
             else:
                 for half in range(2):
-                    d, s = dst[:, :, :, 2 * half : 2 * half + 2], src[:, :, :, 2 * half : 2 * half + 2]
+                    d, s = dst[:, half], src[:, half]
                     if half in vector_halves:
                         nc.vector.tensor_copy(out=d, in_=s)
                     else:
@@ -172,8 +176,10 @@ def tile_moe_tk_glu_sigmoid_kernel(
 
         def prepare_w2(c, hh, on_vector):
             raw = raws["w2", c, hh]
-            if hh == 1 and c == 2:
+            if hh == 1 and c > 0:
                 grouped = held.tile([P, H * PACK], BF16, name="late_grouped", tag=f"late{c}", align_bytes=64)
+            elif c == 2:
+                grouped = held.tile([P, H * PACK], BF16, name="mid_grouped", tag="x_grouped", align_bytes=64)
             else:
                 grouped = grp.tile([P, H * PACK], BF16, name="grouped", align_bytes=64)
             for q in range(4):
@@ -207,10 +213,11 @@ def tile_moe_tk_glu_sigmoid_kernel(
                             start=True,
                             stop=True,
                         )
-                    accs.append(acc[:].rearrange("p t s -> p s t"))
-                sig = host[:, s + row, :].rearrange("p (s t) -> p s t", t=PACK)
+                    accs.append(acc[:].rearrange("p t (c i) -> p c t i", i=2))
+                sig = host[:, s + row, :].rearrange("p (c t i) -> p c t i", t=PACK, i=2)
                 nc.scalar.activation(sig, accs[0], SIGMOID)
-                nc.vector.tensor_tensor(h_grouped[:, slots, :], sig, accs[1], MULT)
+                h_out = h_grouped[:, slots, :].rearrange("p (c i) t -> p c t i", i=2)
+                nc.vector.tensor_tensor(h_out, sig, accs[1], MULT)
             hidden[e] = h_grouped
 
         def quantize_hidden(e):
@@ -244,20 +251,29 @@ def tile_moe_tk_glu_sigmoid_kernel(
                         )
                     nc.scalar.copy(out=y_rows[c][:, 2 * pair * C : 2 * (pair + 1) * C], in_=acc[:])
 
-        def combine(c):
-            if c == 1:
-                first = held.tile([P, 4, T], F32, name="first", tag="apart")
-                second = held.tile([P, 2, T], F32, name="second", tag="late2", align_bytes=64)
+        def gated(c):
+            if c == 0:
+                first = prodp.tile([P, R, T], F32, name="prods")
+                second = held.tile([P, 2, T], F32, name="second", tag="late1", align_bytes=64)
                 prods = [first[:, 0, :], first[:, 1, :], second[:, 0, :], second[:, 1, :]]
+            elif c == 1:
+                first = rawp.tile([P, 4, T], F32, name="raw")
+                second = held.tile([P, 2, T], F32, name="second", tag="late2", align_bytes=64)
+                middle = held.tile([P, 2, T], F32, name="middle", tag="x_grouped", align_bytes=64)
+                prods = [first[:, 0, :], middle[:, 0, :], middle[:, 1, :], second[:, 0, :]]
             else:
                 whole = prodp.tile([P, R, T], F32, name="prods")
                 prods = [whole[:, r, :] for r in range(R)]
             for r in range(R):
                 nc.vector.tensor_tensor(prods[r], y_rows[c][:].indirect(pos_t[r][:]), gates[:, r, :], MULT)
+            products[c] = prods
+
+        def add_up(c):
+            prods = products[c]
             rows = out[c * P : (c + 1) * P, :]
             last = c == NCHUNKS - 1
             terms = 2 if last else R
-            turned = psy.tile([P, 2 * C], F32, name="acc_y")
+            turned = psg.tile([P, T], F32, name="acc_w3")
             for r in range(terms):
                 for b in range(T // P):
                     cols = slice(b * P, (b + 1) * P)
@@ -269,7 +285,10 @@ def tile_moe_tk_glu_sigmoid_kernel(
                         stop=r == terms - 1 and b == T // P - 1,
                         is_transpose=True,
                     )
-            turned_sb = work.tile([P, T], F32, name="turned_sb")
+            if c == 0:
+                turned_sb = held.tile([P, T], F32, name="turned_late", tag="apart")
+            else:
+                turned_sb = work.tile([P, T], F32, name="turned_sb")
             nc.scalar.copy(out=turned_sb[:], in_=turned[:])
             back = psa.tile([P, T], F32, name="acc_w1")
             for b in range(T // P):
@@ -286,10 +305,10 @@ def tile_moe_tk_glu_sigmoid_kernel(
                     nc.vector.tensor_tensor(sums[:, cols], prods[2][:, cols], back[:, cols], ADD)
                     nc.sync.dma_start(out=rows[:, cols], in_=sums[:, cols])
 
+        for g in range(E // GROUP):
+            gather(g)
         for e in range(E):
-            gather(e)
-        for e in range(E):
-            interleave("w3", e, (0, 1) if e >= 3 else ())
+            interleave("w3", e, (0, 1) if e >= 2 else ())
             load_next()
             interleave("w1", e, (0,) if e == E - 1 else ())
             load_next()
@@ -304,15 +323,23 @@ def tile_moe_tk_glu_sigmoid_kernel(
                 first_layer(0)
             if e >= 2:
                 first_layer(e - 1)
+            if e == 7:
+                prepare_w2(0, 1, 0)
             second_layer()
         quantize_hidden(E - 2)
         first_layer(E - 1)
-        prepare_w2(0, 1, 0)
         quantize_hidden(E - 1)
         second_layer()
-        for c in range(1, NCHUNKS):
-            for hh in range(2):
-                prepare_w2(c, hh, 4 if (c, hh) == (2, 0) else 0)
-                second_layer()
-            combine(c - 1)
-        combine(NCHUNKS - 1)
+        for hh in range(2):
+            prepare_w2(1, hh, 4 if hh == 0 else 0)
+            second_layer()
+        gated(0)
+        prepare_w2(2, 0, 0)
+        add_up(0)
+        second_layer()
+        prepare_w2(2, 1, 2)
+        second_layer()
+        gated(1)
+        add_up(1)
+        gated(2)
+        add_up(2)

@@ -56,15 +56,19 @@ def tile_moe_tk_glu_sigmoid_kernel(
         nc.gpsimd.memset(x_scales[:].bitcast(U32), 0)
         nc.gpsimd.memset(x_codes[:, T:], 0)
 
-        x_raw = held.tile([P, PACK, T], F32, name="x_raw", tag="late1", align_bytes=64)
-        nc.sync.dma_start(out=x_raw[:], in_=xT.rearrange("(p j) t -> p j t", j=PACK))
+        x_raw = []
+        for half in range(2):
+            xr = held.tile([P, PACK, T // 2], F32, name="x_raw", tag=f"late{half + 1}", align_bytes=64)
+            tokens = slice(half * (T // 2), (half + 1) * (T // 2))
+            nc.sync.dma_start(out=xr[:], in_=xT[:, tokens].rearrange("(p j) t -> p j t", j=PACK))
+            x_raw.append(xr)
         offs_t = held.tile([P, S // 16], U16, name="offs_t")
         nc.sync.dma_start(offs_t[:], offs)
 
         raws = {}
         loads = []
         for e in range(E):
-            loads += [("w3", e, 0), ("w1", e, 0)]
+            loads += [("w3", e, 0), ("w1", e, 0)] if e < E - 1 else [("w1", e, 0), ("w3", e, 0)]
             if e == 5:
                 loads += [("w2", 0, 0)]
         loads += [("w2", 0, 1), ("w2", 1, 0), ("w2", 1, 1), ("w2", 2, 0), ("w2", 2, 1)]
@@ -74,9 +78,9 @@ def tile_moe_tk_glu_sigmoid_kernel(
                 return
             kind, i, hh = loads.pop(0)
             if (kind, i, hh) in (("w2", 0, 0), ("w2", 2, 0)):
-                raw = held.tile([P, 4, T], F32, name="raw_apart", tag="apart")
+                raw = held.tile([P, 4, T], F32, name="raw_apart", tag="apart", align_bytes=64)
             else:
-                raw = rawp.tile([P, 4, T], F32, name="raw")
+                raw = rawp.tile([P, 4, T], F32, name="raw", align_bytes=64)
             if kind == "w1":
                 nc.sync.dma_start(out=raw[:], in_=w1[i, :, :].rearrange("(p j) h -> p j h", j=PACK))
             elif kind == "w3":
@@ -116,18 +120,25 @@ def tile_moe_tk_glu_sigmoid_kernel(
                 nc.scalar.activation(dst, src, COPY)
 
         x_grouped = held.tile([P, T * PACK], BF16, name="x_grouped", tag="x_grouped", align_bytes=64)
-        plain_copy(True, x_grouped[:], x_raw[:])
-        nc.vector.quantize_mx(out=x_codes[:, :T].bitcast(FP8X4), scales=x_scales[:, :T], in_=x_grouped[:])
+        for half in range(2):
+            tokens = slice(half * (T // 2), (half + 1) * (T // 2))
+            part = x_grouped[:, half * (T // 2) * PACK : (half + 1) * (T // 2) * PACK]
+            plain_copy(True, part, x_raw[half][:])
+            nc.vector.quantize_mx(out=x_codes[:, tokens].bitcast(FP8X4), scales=x_scales[:, tokens], in_=part)
 
         y_rows = []
         for c in range(NCHUNKS):
             yt = held.tile([P, S], F32, name=f"y_rows{c}")
             y_rows.append(yt)
-        weights, gathered, h_codes, w2_codes, pairs, hidden, products = {}, {}, {}, {}, {}, {}, {}
+        weights, gathered, h_codes, w2_codes, pairs, hidden, products, banks = {}, {}, {}, {}, {}, {}, {}, {}
+        w2_grouped = {}
         y_done = []
 
-        def quantize(grouped):
-            codes = codep.tile([P, H], U32, name="w2_codes", align_bytes=64)
+        def quantize(grouped, apart):
+            if apart:
+                codes = held.tile([P, H], U32, name="codes_apart", tag="apart", align_bytes=64)
+            else:
+                codes = codep.tile([P, H], U32, name="w2_codes", align_bytes=64)
             scales = codep.tile([P, H], U8, name="w2_scales", align_bytes=64)
             nc.vector.quantize_mx(out=codes[:].bitcast(FP8X4), scales=scales[:], in_=grouped[:])
             return codes, scales
@@ -168,7 +179,7 @@ def tile_moe_tk_glu_sigmoid_kernel(
                     out=codes[:].bitcast(FP8X4), scales=scales[:], in_=pairs[e][:].rearrange("p k c -> p (k c)")
                 )
             else:
-                for k in (1, 0):
+                for k in range(2):
                     cols = slice(k * H, (k + 1) * H)
                     nc.vector.quantize_mx(out=codes[:, cols].bitcast(FP8X4), scales=scales[:, cols], in_=pairs[e][:, k, :])
             weights["w1", e] = (codes[:, 0:H], scales[:, 0:H])
@@ -188,20 +199,29 @@ def tile_moe_tk_glu_sigmoid_kernel(
                     grouped[:, q * 512 : (q + 1) * 512],
                     raw[:, q, :].rearrange("p (j n) -> p j n", j=PACK),
                 )
-            w2_codes[c, hh] = quantize(grouped)
+            w2_grouped[c, hh] = grouped
+
+        def quantize_w2(c, hh):
+            w2_codes[c, hh] = quantize(w2_grouped[c, hh], (c, hh) == (2, 1))
 
         def first_layer(e):
             g_codes, g_scales = gathered.pop(e)
-            if e == E - 1:
-                host, row = held.tile([P, 2, T], F32, name="last_sig", tag="x_grouped", align_bytes=64), 0
+            if e in (5, 7):
+                host, row = raws["w1", e, 0], 2
             else:
-                host, row = (raws["w1", 2, 0], 2 * e) if e < 2 else (raws["w1", e + 1, 0], 0)
-            h_grouped = work.tile([P, C, PACK], BF16, name="h_grouped", align_bytes=64)
+                host, row = raws["w1", e + 1, 0], 0
+            if e == E - 2:
+                h_grouped = raws["w3", E - 1, 0][:, 0, :].bitcast(BF16).rearrange("p (s t) -> p s t", t=PACK)
+            else:
+                h_grouped = work.tile([P, C, PACK], BF16, name="h_grouped", align_bytes=64)
             for s in range(C // P):
                 slots = slice(s * P, (s + 1) * P)
                 accs = []
                 for kind, pool in (("w1", psa), ("w3", psg)):
-                    acc = pool.tile([P, PACK, P], F32, name=f"acc_{kind}")
+                    if kind == "w1" and e == E - 1:
+                        acc = psy.tile([P, PACK, P], F32, name="acc_y")
+                    else:
+                        acc = pool.tile([P, PACK, P], F32, name=f"acc_{kind}")
                     codes, scales = weights[kind, e]
                     for t in range(PACK):
                         nc.tensor.matmul_mx(
@@ -257,7 +277,7 @@ def tile_moe_tk_glu_sigmoid_kernel(
                 second = held.tile([P, 2, T], F32, name="second", tag="late1", align_bytes=64)
                 prods = [first[:, 0, :], first[:, 1, :], second[:, 0, :], second[:, 1, :]]
             elif c == 1:
-                first = rawp.tile([P, 4, T], F32, name="raw")
+                first = rawp.tile([P, 4, T], F32, name="raw", align_bytes=64)
                 second = held.tile([P, 2, T], F32, name="second", tag="late2", align_bytes=64)
                 middle = held.tile([P, 2, T], F32, name="middle", tag="x_grouped", align_bytes=64)
                 prods = [first[:, 0, :], middle[:, 0, :], middle[:, 1, :], second[:, 0, :]]
@@ -268,11 +288,9 @@ def tile_moe_tk_glu_sigmoid_kernel(
                 nc.vector.tensor_tensor(prods[r], y_rows[c][:].indirect(pos_t[r][:]), gates[:, r, :], MULT)
             products[c] = prods
 
-        def add_up(c):
+        def turn(c):
             prods = products[c]
-            rows = out[c * P : (c + 1) * P, :]
-            last = c == NCHUNKS - 1
-            terms = 2 if last else R
+            terms = 2 if c == NCHUNKS - 1 else R
             turned = psg.tile([P, T], F32, name="acc_w3")
             for r in range(terms):
                 for b in range(T // P):
@@ -285,8 +303,14 @@ def tile_moe_tk_glu_sigmoid_kernel(
                         stop=r == terms - 1 and b == T // P - 1,
                         is_transpose=True,
                     )
+            banks[c] = turned
+
+        def add_up(c):
+            prods, turned = products[c], banks[c]
+            rows = out[c * P : (c + 1) * P, :]
+            last = c == NCHUNKS - 1
             if c == 0:
-                turned_sb = held.tile([P, T], F32, name="turned_late", tag="apart")
+                turned_sb = held.tile([P, T], F32, name="turned_late", tag="apart", align_bytes=64)
             else:
                 turned_sb = work.tile([P, T], F32, name="turned_sb")
             nc.scalar.copy(out=turned_sb[:], in_=turned[:])
@@ -310,36 +334,38 @@ def tile_moe_tk_glu_sigmoid_kernel(
         for e in range(E):
             interleave("w3", e, (0, 1) if e >= 2 else ())
             load_next()
-            interleave("w1", e, (0,) if e == E - 1 else ())
+            interleave("w1", e, ())
             load_next()
-            if e == 3:
-                quantize_hidden(0)
-            if e >= 3:
-                quantize_hidden(e - 2)
-            if e == 6:
-                prepare_w2(0, 0, 0)
-            quantize_pair(e)
-            if e == 2:
-                first_layer(0)
             if e >= 2:
+                quantize_hidden(e - 2)
+            quantize_pair(e)
+            if e >= 1:
                 first_layer(e - 1)
-            if e == 7:
-                prepare_w2(0, 1, 0)
-            second_layer()
-        quantize_hidden(E - 2)
+            if e == 5:
+                prepare_w2(0, 0, 0)
+                quantize_w2(0, 0)
         first_layer(E - 1)
+        quantize_hidden(E - 2)
+        prepare_w2(0, 1, 0)
+        quantize_w2(0, 1)
         quantize_hidden(E - 1)
         second_layer()
         for hh in range(2):
             prepare_w2(1, hh, 4 if hh == 0 else 0)
+            quantize_w2(1, hh)
             second_layer()
         gated(0)
+        turn(0)
         prepare_w2(2, 0, 0)
-        add_up(0)
+        quantize_w2(2, 0)
         second_layer()
-        prepare_w2(2, 1, 2)
+        prepare_w2(2, 1, 4)
+        quantize_w2(2, 1)
         second_layer()
         gated(1)
+        turn(1)
+        add_up(0)
         add_up(1)
         gated(2)
+        turn(2)
         add_up(2)

@@ -69,15 +69,13 @@ def tile_moe_tk_glu_sigmoid_kernel(
         loads = []
         for e in range(E):
             loads += [("w3", e, 0), ("w1", e, 0)] if e < E - 1 else [("w1", e, 0), ("w3", e, 0)]
-            if e == 5:
-                loads += [("w2", 0, 0)]
-        loads += [("w2", 0, 1), ("w2", 1, 0), ("w2", 1, 1), ("w2", 2, 0), ("w2", 2, 1)]
+        loads += [("w2", 0, 0), ("w2", 0, 1), ("w2", 1, 0), ("w2", 1, 1), ("w2", 2, 0), ("w2", 2, 1)]
 
         def load_next():
             if not loads:
                 return
             kind, i, hh = loads.pop(0)
-            if (kind, i, hh) in (("w2", 0, 0), ("w2", 2, 0)):
+            if (kind, i, hh) in (("w1", 5, 0), ("w2", 2, 0)):
                 raw = held.tile([P, 4, T], F32, name="raw_apart", tag="apart", align_bytes=64)
             else:
                 raw = rawp.tile([P, 4, T], F32, name="raw", align_bytes=64)
@@ -179,9 +177,10 @@ def tile_moe_tk_glu_sigmoid_kernel(
                     out=codes[:].bitcast(FP8X4), scales=scales[:], in_=pairs[e][:].rearrange("p k c -> p (k c)")
                 )
             else:
-                for k in range(2):
-                    cols = slice(k * H, (k + 1) * H)
-                    nc.vector.quantize_mx(out=codes[:, cols].bitcast(FP8X4), scales=scales[:, cols], in_=pairs[e][:, k, :])
+                nc.vector.quantize_mx(out=codes[:, :H].bitcast(FP8X4), scales=scales[:, :H], in_=pairs[e][:, 0, :])
+                first_layer(e - 1)
+                quantize_hidden(e - 1)
+                nc.vector.quantize_mx(out=codes[:, H:].bitcast(FP8X4), scales=scales[:, H:], in_=pairs[e][:, 1, :])
             weights["w1", e] = (codes[:, 0:H], scales[:, 0:H])
             weights["w3", e] = (codes[:, H : 2 * H], scales[:, H : 2 * H])
 
@@ -210,18 +209,12 @@ def tile_moe_tk_glu_sigmoid_kernel(
                 host, row = raws["w1", e, 0], 2
             else:
                 host, row = raws["w1", e + 1, 0], 0
-            if e == E - 2:
-                h_grouped = raws["w3", E - 1, 0][:, 0, :].bitcast(BF16).rearrange("p (s t) -> p s t", t=PACK)
-            else:
-                h_grouped = work.tile([P, C, PACK], BF16, name="h_grouped", align_bytes=64)
+            h_grouped = work.tile([P, C, PACK], BF16, name="h_grouped", align_bytes=64)
             for s in range(C // P):
                 slots = slice(s * P, (s + 1) * P)
                 accs = []
                 for kind, pool in (("w1", psa), ("w3", psg)):
-                    if kind == "w1" and e == E - 1:
-                        acc = psy.tile([P, PACK, P], F32, name="acc_y")
-                    else:
-                        acc = pool.tile([P, PACK, P], F32, name=f"acc_{kind}")
+                    acc = pool.tile([P, PACK, P], F32, name=f"acc_{kind}")
                     codes, scales = weights[kind, e]
                     for t in range(PACK):
                         nc.tensor.matmul_mx(
@@ -334,21 +327,20 @@ def tile_moe_tk_glu_sigmoid_kernel(
         for e in range(E):
             interleave("w3", e, (0, 1) if e >= 2 else ())
             load_next()
-            interleave("w1", e, ())
+            interleave("w1", e, (0,) if e >= E - 2 else ())
             load_next()
             if e >= 2:
                 quantize_hidden(e - 2)
             quantize_pair(e)
-            if e >= 1:
+            if 1 <= e < E - 1:
                 first_layer(e - 1)
-            if e == 5:
-                prepare_w2(0, 0, 0)
-                quantize_w2(0, 0)
         first_layer(E - 1)
-        quantize_hidden(E - 2)
-        prepare_w2(0, 1, 0)
-        quantize_w2(0, 1)
+        prepare_w2(0, 0, 0)
+        quantize_w2(0, 0)
         quantize_hidden(E - 1)
+        second_layer()
+        prepare_w2(0, 1, 2)
+        quantize_w2(0, 1)
         second_layer()
         for hh in range(2):
             prepare_w2(1, hh, 4 if hh == 0 else 0)
@@ -359,7 +351,7 @@ def tile_moe_tk_glu_sigmoid_kernel(
         prepare_w2(2, 0, 0)
         quantize_w2(2, 0)
         second_layer()
-        prepare_w2(2, 1, 4)
+        prepare_w2(2, 1, 2)
         quantize_w2(2, 1)
         second_layer()
         gated(1)

@@ -155,15 +155,15 @@ def tile_moe_tk_glu_sigmoid_kernel(
             if kind == "w3":
                 pairs[e] = grp.tile([P, 2, H * PACK], BF16, name="grouped", align_bytes=64)
             grouped = pairs[e][:, 0 if kind == "w1" else 1, :]
-            src = raw[:].rearrange("p j (m u v) -> p u m j v", u=2, v=2)
-            dst = grouped.rearrange("p (u v m j) -> p u m j v", u=2, v=2, j=PACK)
+            src = raw[:].rearrange("p j (m t) -> p m j t", t=PACK)
+            dst = grouped.rearrange("p (t m j) -> p m j t", t=PACK, j=PACK)
             if len(vector_halves) == 2:
                 nc.vector.tensor_copy(out=dst, in_=src)
             elif not vector_halves:
                 nc.scalar.copy(out=dst, in_=src)
             else:
                 for half in range(2):
-                    d, s = dst[:, half], src[:, half]
+                    d, s = dst[:, half * (P // 2) : (half + 1) * (P // 2)], src[:, half * (P // 2) : (half + 1) * (P // 2)]
                     if half in vector_halves:
                         nc.vector.tensor_copy(out=d, in_=s)
                     else:

@@ -6,6 +6,7 @@ from concourse.masks import make_identity
 E, C, T, K, H, N, R = 8, 256, 512, 512, 512, 384, 4
 S = E * C
 FLOPS = 2 * S * (2 * K * H + H * N)
+BYTES = 4 * (K * T + E * (2 * K * H + H * N) + R * T + N * T) + 2 * 128 * (S + R * T) // 16
 
 F32 = mybir.dt.float32
 BF16 = mybir.dt.bfloat16
@@ -20,10 +21,16 @@ ADD = mybir.AluOpType.add
 
 P = 128
 PACK = 4
-NCHUNKS = N // P
-RAW_BUFS = 11
-GROUP = 4
+LIST_ROWS = 16
+CHUNKS = N // P
+HALF = E // 2
+LAST = E - 1
+RING = 11
 WINDOW = 1408
+W3_ON_SCALAR = 2
+W1_SHARED = 2
+LAST_PIECES_ON_VECTOR = 2
+OWN_HOST = LAST - W1_SHARED
 
 
 def tile_moe_tk_glu_sigmoid_kernel(
@@ -32,22 +39,17 @@ def tile_moe_tk_glu_sigmoid_kernel(
     nc = tc.nc
     with ExitStack() as ctx:
         held = ctx.enter_context(tc.tile_pool(name="held", bufs=1))
-        rawp = ctx.enter_context(tc.tile_pool(name="rawp", bufs=RAW_BUFS))
-        grp = ctx.enter_context(tc.tile_pool(name="grp", bufs=3))
-        codep = ctx.enter_context(tc.tile_pool(name="codep", bufs=3))
-        prodp = ctx.enter_context(tc.tile_pool(name="prodp", bufs=1))
+        ring = ctx.enter_context(tc.tile_pool(name="ring", bufs=RING))
+        rounded = ctx.enter_context(tc.tile_pool(name="rounded", bufs=3))
+        quantised = ctx.enter_context(tc.tile_pool(name="quantised", bufs=3))
+        single = ctx.enter_context(tc.tile_pool(name="single", bufs=1))
         work = ctx.enter_context(tc.tile_pool(name="work", bufs=2))
-        psa = ctx.enter_context(tc.psum_pool(name="psa", bufs=3))
-        psg = ctx.enter_context(tc.psum_pool(name="psg", bufs=3))
-        psy = ctx.enter_context(tc.psum_pool(name="psy", bufs=2))
+        banks_a = ctx.enter_context(tc.psum_pool(name="banks_a", bufs=3))
+        banks_g = ctx.enter_context(tc.psum_pool(name="banks_g", bufs=3))
+        banks_y = ctx.enter_context(tc.psum_pool(name="banks_y", bufs=2))
 
-        warm = held.tile([P, 1], F32, name="warm")
-        warm_out = held.tile([P, 1], F32, name="warm_out")
-        nc.gpsimd.memset(warm[:], 0.0)
-        nc.scalar.activation(warm_out[:], warm[:], SIGMOID)
-
-        gate_cols = held.tile([P, R, PACK], F32, name="gate_cols")
-        nc.scalar.dma_start(out=gate_cols[:], in_=gate[:, 0, :].rearrange("r (q c) -> q r c", c=PACK))
+        gate_cols = held.tile([P, R, T // P], F32, name="gate_cols")
+        nc.scalar.dma_start(out=gate_cols[:], in_=gate[:, 0, :].rearrange("r (q c) -> q r c", q=P))
         ident = held.tile([P, P], F32, name="ident")
         make_identity(nc, ident[:])
 
@@ -56,308 +58,304 @@ def tile_moe_tk_glu_sigmoid_kernel(
         nc.gpsimd.memset(x_scales[:].bitcast(U32), 0)
         nc.gpsimd.memset(x_codes[:, T:], 0)
 
+        token_halves = [slice(half * (T // 2), (half + 1) * (T // 2)) for half in range(2)]
         x_raw = []
-        for half in range(2):
-            xr = held.tile([P, PACK, T // 2], F32, name="x_raw", tag=f"late{half + 1}", align_bytes=64)
-            tokens = slice(half * (T // 2), (half + 1) * (T // 2))
-            nc.sync.dma_start(out=xr[:], in_=xT[:, tokens].rearrange("(p j) t -> p j t", j=PACK))
-            x_raw.append(xr)
-        offs_t = held.tile([P, S // 16], U16, name="offs_t")
+        for half, tokens in enumerate(token_halves):
+            raw_half = held.tile([P, PACK, T // 2], F32, name="x_raw", tag=f"late{half + 1}", align_bytes=64)
+            nc.sync.dma_start(out=raw_half[:], in_=xT[:, tokens].rearrange("(p j) t -> p j t", j=PACK))
+            x_raw.append(raw_half)
+        offs_t = held.tile([P, S // LIST_ROWS], U16, name="offs_t")
         nc.sync.dma_start(offs_t[:], offs)
 
-        raws = {}
         loads = []
         for e in range(E):
-            loads += [("w3", e, 0), ("w1", e, 0)] if e < E - 1 else [("w1", e, 0), ("w3", e, 0)]
-        loads += [("w2", 0, 0), ("w2", 0, 1), ("w2", 1, 0), ("w2", 1, 1), ("w2", 2, 0), ("w2", 2, 1)]
+            loads += [("w3", e), ("w1", e)] if e < LAST else [("w1", e), ("w3", e)]
+        loads += [(c, half) for c in range(CHUNKS) for half in range(2)]
+        apart = (loads[RING], (CHUNKS - 1, 0))
+        raws = {}
 
         def load_next():
             if not loads:
                 return
-            kind, i, hh = loads.pop(0)
-            if (kind, i, hh) in (("w1", 5, 0), ("w2", 2, 0)):
-                raw = held.tile([P, 4, T], F32, name="raw_apart", tag="apart", align_bytes=64)
+            key = loads.pop(0)
+            if key in apart:
+                raw = held.tile([P, PACK, H], F32, name="raw_apart", tag="apart", align_bytes=64)
             else:
-                raw = rawp.tile([P, 4, T], F32, name="raw", align_bytes=64)
-            if kind == "w1":
-                nc.sync.dma_start(out=raw[:], in_=w1[i, :, :].rearrange("(p j) h -> p j h", j=PACK))
-            elif kind == "w3":
-                nc.sync.dma_start(out=raw[:], in_=w3[i, :, :].rearrange("(p j) h -> p j h", j=PACK))
+                raw = ring.tile([P, PACK, H], F32, name="raw", align_bytes=64)
+            if key[0] in ("w1", "w3"):
+                matrix = (w1 if key[0] == "w1" else w3)[key[1], :, :]
+                nc.sync.dma_start(out=raw[:], in_=matrix.rearrange("(p j) h -> p j h", j=PACK))
             else:
-                for q in range(4):
+                c, half = key
+                for q in range(HALF):
                     nc.sync.dma_start(
                         out=raw[:, q, :].rearrange("p (j n) -> p j n", j=PACK),
-                        in_=w2[4 * hh + q, :, i * P : (i + 1) * P].rearrange("(p j) n -> p j n", j=PACK),
+                        in_=w2[HALF * half + q, :, c * P : (c + 1) * P].rearrange("(p j) n -> p j n", j=PACK),
                     )
-            raws[kind, i, hh] = raw
+            raws[key] = raw
 
-        for q in range(RAW_BUFS):
+        for slot in range(RING):
             load_next()
 
         pos_t = []
         for r, pos in enumerate((pos1, pos2, pos3, pos4)):
-            pt = held.tile([P, T // 16], U16, name=f"pos_t{r}")
-            nc.sync.dma_start(pt[:], pos)
-            pos_t.append(pt)
+            list_tile = held.tile([P, T // LIST_ROWS], U16, name=f"pos_t{r}")
+            nc.sync.dma_start(list_tile[:], pos)
+            pos_t.append(list_tile)
 
         gates = held.tile([P, R, T], F32, name="gates")
         for r in range(R):
-            spread = (psa if r % 2 == 0 else psg).tile([P, PACK, P], F32, name="acc_w1" if r % 2 == 0 else "acc_w3")
-            for c in range(PACK):
+            if r % 2 == 0:
+                spread = banks_a.tile([P, T // P, P], F32, name="acc_w1")
+            else:
+                spread = banks_g.tile([P, T // P, P], F32, name="acc_w3")
+            for c in range(T // P):
                 nc.tensor.transpose(spread[:, c, :], gate_cols[:, r, c : c + 1].to_broadcast([P, P]), ident[:])
-            nc.scalar.copy(
-                out=gates[:, r, :].rearrange("p (q c) -> p q c", c=PACK), in_=spread[:].rearrange("p c q -> p q c")
-            )
+            nc.scalar.copy(out=gates[:, r, :].rearrange("p (q c) -> p q c", q=P), in_=spread[:].rearrange("p c q -> p q c"))
 
-        def plain_copy(on_vector, dst, src):
-            src = src.rearrange("p j (c i) -> p c j i", i=4)
-            dst = dst.rearrange("p (c i j) -> p c j i", i=4, j=PACK)
+        def interleave(on_vector, dst, src):
+            src = src.rearrange("p j (c i) -> p c j i", i=PACK)
+            dst = dst.rearrange("p (c i j) -> p c j i", i=PACK, j=PACK)
             if on_vector:
                 nc.vector.tensor_copy(out=dst, in_=src)
             else:
                 nc.scalar.activation(dst, src, COPY)
 
-        x_grouped = held.tile([P, T * PACK], BF16, name="x_grouped", tag="x_grouped", align_bytes=64)
-        for half in range(2):
-            tokens = slice(half * (T // 2), (half + 1) * (T // 2))
-            part = x_grouped[:, half * (T // 2) * PACK : (half + 1) * (T // 2) * PACK]
-            plain_copy(True, part, x_raw[half][:])
-            nc.vector.quantize_mx(out=x_codes[:, tokens].bitcast(FP8X4), scales=x_scales[:, tokens], in_=part)
+        def quantize(codes, scales, values):
+            nc.vector.quantize_mx(out=codes.bitcast(FP8X4), scales=scales, in_=values)
 
-        y_rows = []
-        for c in range(NCHUNKS):
-            yt = held.tile([P, S], F32, name=f"y_rows{c}")
-            y_rows.append(yt)
-        weights, gathered, h_codes, w2_codes, pairs, hidden, products, banks = {}, {}, {}, {}, {}, {}, {}, {}
-        w2_grouped = {}
-        y_done = []
+        def multiply(acc, stationary, moving):
+            nc.tensor.matmul_mx(
+                out=acc,
+                lhsT=stationary[0].bitcast(FP8X4),
+                lhsT_scale=stationary[1],
+                rhs=moving[0].bitcast(FP8X4),
+                rhs_scale=moving[1],
+                start=True,
+                stop=True,
+            )
 
-        def quantize(grouped, apart):
-            if apart:
-                codes = held.tile([P, H], U32, name="codes_apart", tag="apart", align_bytes=64)
-            else:
-                codes = codep.tile([P, H], U32, name="w2_codes", align_bytes=64)
-            scales = codep.tile([P, H], U8, name="w2_scales", align_bytes=64)
-            nc.vector.quantize_mx(out=codes[:].bitcast(FP8X4), scales=scales[:], in_=grouped[:])
+        x_rounded = held.tile([P, T * PACK], BF16, name="x_rounded", tag="middle", align_bytes=64)
+        for half, tokens in enumerate(token_halves):
+            values = x_rounded[:, tokens.start * PACK : tokens.stop * PACK]
+            interleave(True, values, x_raw[half][:])
+            quantize(x_codes[:, tokens], x_scales[:, tokens], values)
+
+        y_rows = [held.tile([P, S], F32, name=f"y_rows{c}") for c in range(CHUNKS)]
+        slots_mx, w13_rounded, w13_mx, h_rounded, h_mx = {}, {}, {}, {}, {}
+        w2_rounded, w2_mx, products, turned = {}, {}, {}, {}
+
+        def gather_tokens(half):
+            entries = offs_t[:, half * (HALF * C // LIST_ROWS) : (half + 1) * (HALF * C // LIST_ROWS)]
+            codes = held.tile([P, HALF * C], U32, name=f"slot_codes{half}", align_bytes=64)
+            scales = held.tile([P, HALF * C], U8, name=f"slot_scales{half}", align_bytes=64)
+            nc.vector.tensor_copy(codes[:], x_codes[:].indirect(entries))
+            nc.vector.tensor_copy(scales[:], x_scales[:].indirect(entries))
+            for q in range(HALF):
+                slots_mx[HALF * half + q] = (codes[:, q * C : (q + 1) * C], scales[:, q * C : (q + 1) * C])
+
+        def round_w13(kind, e, engines):
+            if kind == "w3":
+                w13_rounded[e] = rounded.tile([P, 2, H * PACK], BF16, name="w_rounded", align_bytes=64)
+            src = raws[kind, e][:].rearrange("p j (m t) -> p m j t", t=PACK)
+            dst = w13_rounded[e][:, 0 if kind == "w1" else 1, :].rearrange("p (t m j) -> p m j t", t=PACK, j=PACK)
+            for part, engine in enumerate(engines):
+                ms = slice(part * P // len(engines), (part + 1) * P // len(engines))
+                if engine == "vector":
+                    nc.vector.tensor_copy(out=dst[:, ms], in_=src[:, ms])
+                else:
+                    nc.scalar.copy(out=dst[:, ms], in_=src[:, ms])
+
+        def allocate_w13(e):
+            codes = quantised.tile([P, 2 * H], U32, name="w13_codes", align_bytes=64)
+            scales = quantised.tile([P, 2 * H], U8, name="w13_scales", align_bytes=64)
+            w13_mx[e] = (codes, scales)
             return codes, scales
 
-        def gather(g):
-            cols = slice(g * (GROUP * C // 16), (g + 1) * (GROUP * C // 16))
-            g_codes = held.tile([P, GROUP * C], U32, name=f"g_codes{g}", align_bytes=64)
-            g_scales = held.tile([P, GROUP * C], U8, name=f"g_scales{g}", align_bytes=64)
-            nc.vector.tensor_copy(g_codes[:], x_codes[:].indirect(offs_t[:, cols]))
-            nc.vector.tensor_copy(g_scales[:], x_scales[:].indirect(offs_t[:, cols]))
-            for q in range(GROUP):
-                gathered[GROUP * g + q] = (g_codes[:, q * C : (q + 1) * C], g_scales[:, q * C : (q + 1) * C])
-
-        def interleave(kind, e, vector_halves):
-            raw = raws[kind, e, 0]
-            if kind == "w3":
-                pairs[e] = grp.tile([P, 2, H * PACK], BF16, name="grouped", align_bytes=64)
-            grouped = pairs[e][:, 0 if kind == "w1" else 1, :]
-            src = raw[:].rearrange("p j (m t) -> p m j t", t=PACK)
-            dst = grouped.rearrange("p (t m j) -> p m j t", t=PACK, j=PACK)
-            if len(vector_halves) == 2:
-                nc.vector.tensor_copy(out=dst, in_=src)
-            elif not vector_halves:
-                nc.scalar.copy(out=dst, in_=src)
-            else:
-                for half in range(2):
-                    d, s = dst[:, half * (P // 2) : (half + 1) * (P // 2)], src[:, half * (P // 2) : (half + 1) * (P // 2)]
-                    if half in vector_halves:
-                        nc.vector.tensor_copy(out=d, in_=s)
-                    else:
-                        nc.scalar.copy(out=d, in_=s)
-
-        def quantize_pair(e):
-            codes = codep.tile([P, 2 * H], U32, name="codes", align_bytes=64)
-            scales = codep.tile([P, 2 * H], U8, name="scales", align_bytes=64)
-            if e < E - 1:
-                nc.vector.quantize_mx(
-                    out=codes[:].bitcast(FP8X4), scales=scales[:], in_=pairs[e][:].rearrange("p k c -> p (k c)")
-                )
-            else:
-                nc.vector.quantize_mx(out=codes[:, :H].bitcast(FP8X4), scales=scales[:, :H], in_=pairs[e][:, 0, :])
-                first_layer(e - 1)
-                quantize_hidden(e - 1)
-                nc.vector.quantize_mx(out=codes[:, H:].bitcast(FP8X4), scales=scales[:, H:], in_=pairs[e][:, 1, :])
-            weights["w1", e] = (codes[:, 0:H], scales[:, 0:H])
-            weights["w3", e] = (codes[:, H : 2 * H], scales[:, H : 2 * H])
-
-        def prepare_w2(c, hh, on_vector):
-            raw = raws["w2", c, hh]
-            if hh == 1 and c > 0:
-                grouped = held.tile([P, H * PACK], BF16, name="late_grouped", tag=f"late{c}", align_bytes=64)
-            elif c == 2:
-                grouped = held.tile([P, H * PACK], BF16, name="mid_grouped", tag="x_grouped", align_bytes=64)
-            else:
-                grouped = grp.tile([P, H * PACK], BF16, name="grouped", align_bytes=64)
-            for q in range(4):
-                plain_copy(
-                    q >= 4 - on_vector,
-                    grouped[:, q * 512 : (q + 1) * 512],
-                    raw[:, q, :].rearrange("p (j n) -> p j n", j=PACK),
-                )
-            w2_grouped[c, hh] = grouped
-
-        def quantize_w2(c, hh):
-            w2_codes[c, hh] = quantize(w2_grouped[c, hh], (c, hh) == (2, 1))
-
         def first_layer(e):
-            g_codes, g_scales = gathered.pop(e)
-            if e in (5, 7):
-                host, row = raws["w1", e, 0], 2
+            if e in (OWN_HOST, LAST):
+                host = raws["w1", e][:, 2:4, :]
             else:
-                host, row = raws["w1", e + 1, 0], 0
-            h_grouped = work.tile([P, C, PACK], BF16, name="h_grouped", align_bytes=64)
+                host = raws["w1", e + 1][:, 0:2, :]
+            if e == LAST:
+                h = held.tile([P, C, PACK], BF16, name="last_h", tag="middle", align_bytes=64)
+            else:
+                h = work.tile([P, C, PACK], BF16, name="h", align_bytes=64)
+            w_codes, w_scales = w13_mx[e]
+            slot_codes, slot_scales = slots_mx[e]
             for s in range(C // P):
                 slots = slice(s * P, (s + 1) * P)
-                accs = []
-                for kind, pool in (("w1", psa), ("w3", psg)):
-                    acc = pool.tile([P, PACK, P], F32, name=f"acc_{kind}")
-                    codes, scales = weights[kind, e]
+                sums = []
+                for k, (kind, banks) in enumerate((("w1", banks_a), ("w3", banks_g))):
+                    acc = banks.tile([P, PACK, P], F32, name=f"acc_{kind}")
                     for t in range(PACK):
-                        nc.tensor.matmul_mx(
-                            out=acc[:, t, :],
-                            lhsT=codes[:, t * P : (t + 1) * P].bitcast(FP8X4),
-                            lhsT_scale=scales[:, t * P : (t + 1) * P],
-                            rhs=g_codes[:, slots].bitcast(FP8X4),
-                            rhs_scale=g_scales[:, slots],
-                            start=True,
-                            stop=True,
+                        cols = slice(k * H + t * P, k * H + (t + 1) * P)
+                        multiply(
+                            acc[:, t, :],
+                            (w_codes[:, cols], w_scales[:, cols]),
+                            (slot_codes[:, slots], slot_scales[:, slots]),
                         )
-                    accs.append(acc[:].rearrange("p t (c i) -> p c t i", i=2))
-                sig = host[:, s + row, :].rearrange("p (c t i) -> p c t i", t=PACK, i=2)
-                nc.scalar.activation(sig, accs[0], SIGMOID)
-                h_out = h_grouped[:, slots, :].rearrange("p (c i) t -> p c t i", i=2)
-                nc.vector.tensor_tensor(h_out, sig, accs[1], MULT)
-            hidden[e] = h_grouped
+                    sums.append(acc[:].rearrange("p t (c i) -> p c t i", i=2))
+                sig = host[:, s, :].rearrange("p (c t i) -> p c t i", t=PACK, i=2)
+                nc.scalar.activation(sig, sums[0], SIGMOID)
+                nc.vector.tensor_tensor(h[:, slots, :].rearrange("p (c i) t -> p c t i", i=2), sig, sums[1], MULT)
+            h_rounded[e] = h
 
-        def quantize_hidden(e):
-            hc = held.tile([P, C], U32, name=f"h_codes{e}", align_bytes=64)
-            hs = held.tile([P, C], U8, name=f"h_scales{e}", align_bytes=64)
-            nc.vector.quantize_mx(
-                out=hc[:].bitcast(FP8X4), scales=hs[:], in_=hidden[e][:].rearrange("p s t -> p (s t)")
-            )
-            h_codes[e] = (hc, hs)
+        def quantize_h(e):
+            codes = held.tile([P, C], U32, name=f"h_codes{e}", align_bytes=64)
+            scales = held.tile([P, C], U8, name=f"h_scales{e}", align_bytes=64)
+            quantize(codes[:], scales[:], h_rounded[e][:].rearrange("p s t -> p (s t)"))
+            h_mx[e] = (codes, scales)
 
-        def second_layer():
-            for c in range(NCHUNKS):
-                for pair in range(E // 2):
-                    if (c, pair) in y_done or (c, pair // 2) not in w2_codes or 2 * pair + 1 not in h_codes:
-                        continue
-                    y_done.append((c, pair))
-                    codes, scales = w2_codes[c, pair // 2]
-                    acc = psy.tile([P, 2 * C], F32, name="acc_y")
-                    for q in range(2):
-                        e = 2 * pair + q
-                        wcols = slice((e % 4) * P, (e % 4 + 1) * P)
-                        hc, hs = h_codes[e]
-                        nc.tensor.matmul_mx(
-                            out=acc[:, q * C : (q + 1) * C],
-                            lhsT=codes[:, wcols].bitcast(FP8X4),
-                            lhsT_scale=scales[:, wcols],
-                            rhs=hc[:].bitcast(FP8X4),
-                            rhs_scale=hs[:],
-                            start=True,
-                            stop=True,
-                        )
-                    nc.scalar.copy(out=y_rows[c][:, 2 * pair * C : 2 * (pair + 1) * C], in_=acc[:])
-
-        def gated(c):
-            if c == 0:
-                first = prodp.tile([P, R, T], F32, name="prods")
-                second = held.tile([P, 2, T], F32, name="second", tag="late1", align_bytes=64)
-                prods = [first[:, 0, :], first[:, 1, :], second[:, 0, :], second[:, 1, :]]
+        def round_w2(c, half, pieces_on_vector):
+            if half == 1 and c > 0:
+                values = held.tile([P, H * PACK], BF16, name="late_w2", tag=f"late{c}", align_bytes=64)
             elif c == 1:
-                first = rawp.tile([P, 4, T], F32, name="raw", align_bytes=64)
-                second = held.tile([P, 2, T], F32, name="second", tag="late2", align_bytes=64)
-                middle = held.tile([P, 2, T], F32, name="middle", tag="x_grouped", align_bytes=64)
-                prods = [first[:, 0, :], middle[:, 0, :], middle[:, 1, :], second[:, 0, :]]
+                values = single.tile([P, H * PACK], BF16, name="first_products", align_bytes=64)
+            elif half == 0:
+                values = held.tile([P, H * PACK], BF16, name="middle_w2", tag="middle", align_bytes=64)
             else:
-                whole = prodp.tile([P, R, T], F32, name="prods")
-                prods = [whole[:, r, :] for r in range(R)]
-            for r in range(R):
-                nc.vector.tensor_tensor(prods[r], y_rows[c][:].indirect(pos_t[r][:]), gates[:, r, :], MULT)
-            products[c] = prods
+                values = rounded.tile([P, H * PACK], BF16, name="w_rounded", align_bytes=64)
+            for q in range(HALF):
+                interleave(
+                    q >= HALF - pieces_on_vector,
+                    values[:, q * P * PACK : (q + 1) * P * PACK],
+                    raws[c, half][:, q, :].rearrange("p (j n) -> p j n", j=PACK),
+                )
+            w2_rounded[c, half] = values
 
-        def turn(c):
-            prods = products[c]
-            terms = 2 if c == NCHUNKS - 1 else R
-            turned = psg.tile([P, T], F32, name="acc_w3")
-            for r in range(terms):
-                for b in range(T // P):
-                    cols = slice(b * P, (b + 1) * P)
+        def quantize_w2(c, half):
+            if (c, half) == (0, 1):
+                codes = held.tile([P, HALF * P], U32, name="late_codes", tag="late1", align_bytes=64)
+            elif (c, half) == (CHUNKS - 1, 1):
+                codes = held.tile([P, HALF * P], U32, name="last_codes", tag="apart", align_bytes=64)
+            else:
+                codes = quantised.tile([P, HALF * P], U32, name="w2_codes", align_bytes=64)
+            scales = quantised.tile([P, HALF * P], U8, name="w2_scales", align_bytes=64)
+            parts = 1 + half
+            for part in range(parts):
+                words = slice(part * HALF * P // parts, (part + 1) * HALF * P // parts)
+                values = w2_rounded[c, half][:, words.start * PACK : words.stop * PACK]
+                quantize(codes[:, words], scales[:, words], values)
+            w2_mx[c, half] = (codes, scales)
+
+        def second_layer(c, half):
+            codes, scales = w2_mx[c, half]
+            for pair in range(HALF // 2):
+                acc = banks_y.tile([P, 2 * C], F32, name="acc_y")
+                first = HALF * half + 2 * pair
+                for q in range(2):
+                    cols = slice((2 * pair + q) * P, (2 * pair + q + 1) * P)
+                    h_codes, h_scales = h_mx[first + q]
+                    multiply(acc[:, q * C : (q + 1) * C], (codes[:, cols], scales[:, cols]), (h_codes[:], h_scales[:]))
+                nc.scalar.copy(out=y_rows[c][:, first * C : (first + 2) * C], in_=acc[:])
+
+        def gather_results(c):
+            if c == 0:
+                early = single.tile([P, R, T], F32, name="first_products", align_bytes=64)
+                late = held.tile([P, 2, T], F32, name="late_products", tag="late1", align_bytes=64)
+                terms = [early[:, 0, :], early[:, 1, :], late[:, 0, :], late[:, 1, :]]
+            elif c == 1:
+                early = ring.tile([P, PACK, H], F32, name="raw", align_bytes=64)
+                late = held.tile([P, 2, T], F32, name="late_products", tag="late2", align_bytes=64)
+                middle = held.tile([P, 2, T], F32, name="middle_products", tag="middle", align_bytes=64)
+                terms = [early[:, 0, :], middle[:, 0, :], middle[:, 1, :], late[:, 0, :]]
+            else:
+                early = single.tile([P, R, T], F32, name="first_products", align_bytes=64)
+                terms = [early[:, r, :] for r in range(R)]
+            for r in range(R):
+                nc.vector.tensor_tensor(terms[r], y_rows[c][:].indirect(pos_t[r][:]), gates[:, r, :], MULT)
+            products[c] = terms
+
+        blocks = [slice(b * P, (b + 1) * P) for b in range(T // P)]
+
+        def add_turned(c, count):
+            acc = banks_g.tile([P, T], F32, name="acc_w3")
+            for r in range(count):
+                for cols in blocks:
                     nc.tensor.matmul(
-                        turned[:, cols],
-                        lhsT=prods[r][:, cols],
+                        acc[:, cols],
+                        lhsT=products[c][r][:, cols],
                         rhs=ident[:],
-                        start=r == 0 and b == 0,
-                        stop=r == terms - 1 and b == T // P - 1,
+                        start=r == 0 and cols.start == 0,
+                        stop=r == count - 1 and cols.stop == T,
                         is_transpose=True,
                     )
-            banks[c] = turned
+            turned[c] = acc
 
-        def add_up(c):
-            prods, turned = products[c], banks[c]
-            rows = out[c * P : (c + 1) * P, :]
-            last = c == NCHUNKS - 1
+        def turn_back(c):
             if c == 0:
-                turned_sb = held.tile([P, T], F32, name="turned_late", tag="apart", align_bytes=64)
+                staged = held.tile([P, T], F32, name="staged_late", tag="apart", align_bytes=64)
             else:
-                turned_sb = work.tile([P, T], F32, name="turned_sb")
-            nc.scalar.copy(out=turned_sb[:], in_=turned[:])
-            back = psa.tile([P, T], F32, name="acc_w1")
-            for b in range(T // P):
-                cols = slice(b * P, (b + 1) * P)
-                nc.tensor.transpose(back[:, cols], turned_sb[:, cols], ident[:])
-            sums = work.tile([P, T], F32, name="sums")
-            if not last:
-                nc.scalar.copy(out=sums[:], in_=back[:])
-                nc.sync.dma_start(out=rows, in_=sums[:])
-            else:
-                nc.vector.tensor_tensor(prods[2], prods[2], prods[3], ADD)
-                for half in range(2):
-                    cols = slice(half * (T // 2), (half + 1) * (T // 2))
-                    nc.vector.tensor_tensor(sums[:, cols], prods[2][:, cols], back[:, cols], ADD)
-                    nc.sync.dma_start(out=rows[:, cols], in_=sums[:, cols])
+                staged = work.tile([P, T], F32, name="staged")
+            nc.scalar.copy(out=staged[:], in_=turned[c][:])
+            back = banks_a.tile([P, T], F32, name="acc_w1")
+            for cols in blocks:
+                nc.tensor.transpose(back[:, cols], staged[:, cols], ident[:])
+            return back
 
-        for g in range(E // GROUP):
-            gather(g)
+        def store_chunk(c):
+            back = turn_back(c)
+            result = work.tile([P, T], F32, name="result")
+            nc.scalar.copy(out=result[:], in_=back[:])
+            nc.sync.dma_start(out=out[c * P : (c + 1) * P, :], in_=result[:])
+
+        def store_last_chunk():
+            c = CHUNKS - 1
+            back = turn_back(c)
+            result = work.tile([P, T], F32, name="result")
+            terms = products[c]
+            nc.vector.tensor_tensor(terms[2], terms[2], terms[3], ADD)
+            for tokens in token_halves:
+                nc.vector.tensor_tensor(result[:, tokens], terms[2][:, tokens], back[:, tokens], ADD)
+                nc.sync.dma_start(out=out[c * P : (c + 1) * P, tokens], in_=result[:, tokens])
+
+        for half in range(2):
+            gather_tokens(half)
+
         for e in range(E):
-            interleave("w3", e, (0, 1) if e >= 2 else ())
+            round_w13("w3", e, ("scalar",) if e < W3_ON_SCALAR else ("vector",))
             load_next()
-            interleave("w1", e, (0,) if e >= E - 2 else ())
+            round_w13("w1", e, ("vector", "scalar") if e >= E - W1_SHARED else ("scalar",))
             load_next()
             if e >= 2:
-                quantize_hidden(e - 2)
-            quantize_pair(e)
-            if 1 <= e < E - 1:
+                quantize_h(e - 2)
+            codes, scales = allocate_w13(e)
+            if e < LAST:
+                quantize(codes[:], scales[:], w13_rounded[e][:].rearrange("p k c -> p (k c)"))
+                if e >= 1:
+                    first_layer(e - 1)
+            else:
+                quantize(codes[:, :H], scales[:, :H], w13_rounded[e][:, 0, :])
                 first_layer(e - 1)
-        first_layer(E - 1)
-        prepare_w2(0, 0, 0)
+                quantize_h(e - 1)
+                quantize(codes[:, H:], scales[:, H:], w13_rounded[e][:, 1, :])
+
+        round_w2(0, 0, 0)
         quantize_w2(0, 0)
-        quantize_hidden(E - 1)
-        second_layer()
-        prepare_w2(0, 1, 2)
+        first_layer(LAST)
+        round_w2(0, 1, 0)
+        quantize_h(LAST)
         quantize_w2(0, 1)
-        second_layer()
-        for hh in range(2):
-            prepare_w2(1, hh, 4 if hh == 0 else 0)
-            quantize_w2(1, hh)
-            second_layer()
-        gated(0)
-        turn(0)
-        prepare_w2(2, 0, 0)
-        quantize_w2(2, 0)
-        second_layer()
-        prepare_w2(2, 1, 2)
-        quantize_w2(2, 1)
-        second_layer()
-        gated(1)
-        turn(1)
-        add_up(0)
-        add_up(1)
-        gated(2)
-        turn(2)
-        add_up(2)
+        second_layer(0, 0)
+        second_layer(0, 1)
+
+        for half in range(2):
+            round_w2(1, half, HALF if half == 0 else 0)
+            quantize_w2(1, half)
+            second_layer(1, half)
+        gather_results(0)
+        add_turned(0, R)
+
+        for half in range(2):
+            round_w2(2, half, LAST_PIECES_ON_VECTOR if half == 1 else 0)
+            quantize_w2(2, half)
+            second_layer(2, half)
+        gather_results(1)
+        add_turned(1, R)
+        store_chunk(0)
+        store_chunk(1)
+
+        gather_results(2)
+        add_turned(2, 2)
+        store_last_chunk()

@@ -15,7 +15,6 @@ U16 = mybir.dt.uint16
 U8 = mybir.dt.uint8
 FP8X4 = mybir.dt.float8_e4m3fn_x4
 SIGMOID = mybir.ActivationFunctionType.Sigmoid
-COPY = mybir.ActivationFunctionType.Copy
 MULT = mybir.AluOpType.mult
 ADD = mybir.AluOpType.add
 
@@ -25,12 +24,14 @@ LIST_ROWS = 16
 CHUNKS = N // P
 HALF = E // 2
 LAST = E - 1
-RING = 11
+WIDE = H * PACK
+ROOM = 4 * PACK * H
+RING = 7
+AHEAD = 5
 WINDOW = 1408
-W3_ON_SCALAR = 2
-W1_SHARED = 2
-LAST_PIECES_ON_VECTOR = 2
-OWN_HOST = LAST - W1_SHARED
+ROUNDED_ROOM = 2 * (E - AHEAD)
+W3_ON_VECTOR = (0, 64, 64, 64, 112, 112, 112, 128)
+PAIRS_ON_VECTOR = ((3,), (0, 1), ())
 
 
 def tile_moe_tk_glu_sigmoid_kernel(
@@ -40,15 +41,16 @@ def tile_moe_tk_glu_sigmoid_kernel(
     with ExitStack() as ctx:
         held = ctx.enter_context(tc.tile_pool(name="held", bufs=1))
         ring = ctx.enter_context(tc.tile_pool(name="ring", bufs=RING))
-        rounded = ctx.enter_context(tc.tile_pool(name="rounded", bufs=3))
-        quantised = ctx.enter_context(tc.tile_pool(name="quantised", bufs=3))
-        single = ctx.enter_context(tc.tile_pool(name="single", bufs=1))
+        placed = ctx.enter_context(tc.tile_pool(name="placed", bufs=1))
         work = ctx.enter_context(tc.tile_pool(name="work", bufs=2))
         banks_a = ctx.enter_context(tc.psum_pool(name="banks_a", bufs=3))
         banks_g = ctx.enter_context(tc.psum_pool(name="banks_g", bufs=3))
         banks_y = ctx.enter_context(tc.psum_pool(name="banks_y", bufs=2))
 
-        gate_cols = held.tile([P, R, T // P], F32, name="gate_cols")
+        def place(shape, dtype, name, room, start=0):
+            return placed.tile(shape, dtype, name=name, offset=room * ROOM + start, align_bytes=64)
+
+        gate_cols = place([P, R, T // P], F32, "gate_cols", ROUNDED_ROOM)
         nc.scalar.dma_start(out=gate_cols[:], in_=gate[:, 0, :].rearrange("r (q c) -> q r c", q=P))
         ident = held.tile([P, P], F32, name="ident")
         make_identity(nc, ident[:])
@@ -61,42 +63,36 @@ def tile_moe_tk_glu_sigmoid_kernel(
         token_halves = [slice(half * (T // 2), (half + 1) * (T // 2)) for half in range(2)]
         x_raw = []
         for half, tokens in enumerate(token_halves):
-            raw_half = held.tile([P, PACK, T // 2], F32, name="x_raw", tag=f"late{half + 1}", align_bytes=64)
+            raw_half = held.tile([P, PACK, T // 2], F32, name="x_raw", tag=("codes0", "scales1")[half], align_bytes=64)
             nc.sync.dma_start(out=raw_half[:], in_=xT[:, tokens].rearrange("(p j) t -> p j t", j=PACK))
             x_raw.append(raw_half)
         offs_t = held.tile([P, S // LIST_ROWS], U16, name="offs_t")
         nc.sync.dma_start(offs_t[:], offs)
 
-        loads = []
-        for e in range(E):
-            loads += [("w3", e), ("w1", e)] if e < LAST else [("w1", e), ("w3", e)]
-        loads += [(c, half) for c in range(CHUNKS) for half in range(2)]
-        apart = (loads[RING], (CHUNKS - 1, 0))
         raws = {}
 
-        def load_next():
-            if not loads:
-                return
-            key = loads.pop(0)
-            if key in apart:
-                raw = held.tile([P, PACK, H], F32, name="raw_apart", tag="apart", align_bytes=64)
-            else:
+        def load_expert(e):
+            for kind, matrix in (("w1", w1), ("w3", w3)):
+                if 1 <= e <= E - AHEAD:
+                    raw = place([P, PACK, H], F32, f"{kind}_{e}", 2 * (e - 1) + (kind == "w3"))
+                else:
+                    raw = ring.tile([P, PACK, H], F32, name="raw", align_bytes=64)
+                nc.sync.dma_start(out=raw[:], in_=matrix[e, :, :].rearrange("(p j) h -> p j h", j=PACK))
+                raws[kind, e] = raw
+
+        def load_half(c, half):
+            if c == 0:
                 raw = ring.tile([P, PACK, H], F32, name="raw", align_bytes=64)
-            if key[0] in ("w1", "w3"):
-                matrix = (w1 if key[0] == "w1" else w3)[key[1], :, :]
-                nc.sync.dma_start(out=raw[:], in_=matrix.rearrange("(p j) h -> p j h", j=PACK))
             else:
-                c, half = key
-                for q in range(HALF):
-                    nc.sync.dma_start(
-                        out=raw[:, q, :].rearrange("p (j n) -> p j n", j=PACK),
-                        in_=w2[HALF * half + q, :, c * P : (c + 1) * P].rearrange("(p j) n -> p j n", j=PACK),
-                    )
-            raws[key] = raw
+                raw = place([P, PACK, H], F32, f"w2_{c}_{half}", 2 * (c - 1) + half)
+            for q in range(HALF):
+                e = HALF * half + q
+                nc.sync.dma_start(out=raw[:, q, :].rearrange("p (j n) -> p j n", j=PACK), in_=w2[e, :, c * P : (c + 1) * P].rearrange("(p j) n -> p j n", j=PACK))
 
-        for slot in range(RING):
-            load_next()
+            raws[c, half] = raw
 
+        for e in range(E - 2):
+            load_expert(e)
         pos_t = []
         for r, pos in enumerate((pos1, pos2, pos3, pos4)):
             list_tile = held.tile([P, T // LIST_ROWS], U16, name=f"pos_t{r}")
@@ -113,13 +109,18 @@ def tile_moe_tk_glu_sigmoid_kernel(
                 nc.tensor.transpose(spread[:, c, :], gate_cols[:, r, c : c + 1].to_broadcast([P, P]), ident[:])
             nc.scalar.copy(out=gates[:, r, :].rearrange("p (q c) -> p q c", q=P), in_=spread[:].rearrange("p c q -> p q c"))
 
-        def interleave(on_vector, dst, src):
-            src = src.rearrange("p j (c i) -> p c j i", i=PACK)
-            dst = dst.rearrange("p (c i j) -> p c j i", i=PACK, j=PACK)
-            if on_vector:
+        def copy_on(engine, dst, src):
+            if engine == "vector":
                 nc.vector.tensor_copy(out=dst, in_=src)
             else:
-                nc.scalar.activation(dst, src, COPY)
+                nc.scalar.copy(out=dst, in_=src)
+
+        def interleave(engine, dst, src):
+            copy_on(
+                engine,
+                dst.rearrange("p (c i j) -> p c j i", i=PACK, j=PACK),
+                src.rearrange("p j (c i) -> p c j i", i=PACK),
+            )
 
         def quantize(codes, scales, values):
             nc.vector.quantize_mx(out=codes.bitcast(FP8X4), scales=scales, in_=values)
@@ -135,58 +136,53 @@ def tile_moe_tk_glu_sigmoid_kernel(
                 stop=True,
             )
 
-        x_rounded = held.tile([P, T * PACK], BF16, name="x_rounded", tag="middle", align_bytes=64)
+        x_rounded = held.tile([P, T * PACK], BF16, name="x_rounded", tag="codes1", align_bytes=64)
         for half, tokens in enumerate(token_halves):
             values = x_rounded[:, tokens.start * PACK : tokens.stop * PACK]
-            interleave(True, values, x_raw[half][:])
+            interleave("vector", values, x_raw[half][:])
             quantize(x_codes[:, tokens], x_scales[:, tokens], values)
 
         y_rows = [held.tile([P, S], F32, name=f"y_rows{c}") for c in range(CHUNKS)]
-        slots_mx, w13_rounded, w13_mx, h_rounded, h_mx = {}, {}, {}, {}, {}
+        slots_mx, w13_mx, sums, h_rounded, h_mx = {}, {}, {}, {}, {}
         w2_rounded, w2_mx, products, turned = {}, {}, {}, {}
 
-        def gather_tokens(half):
-            entries = offs_t[:, half * (HALF * C // LIST_ROWS) : (half + 1) * (HALF * C // LIST_ROWS)]
-            codes = held.tile([P, HALF * C], U32, name=f"slot_codes{half}", align_bytes=64)
-            scales = held.tile([P, HALF * C], U8, name=f"slot_scales{half}", align_bytes=64)
+        def gather_tokens(first, count):
+            entries = offs_t[:, first * (C // LIST_ROWS) : (first + count) * (C // LIST_ROWS)]
+            if first < AHEAD:
+                codes = held.tile([P, count * C], U32, name=f"slot_codes{first}", align_bytes=64)
+                scales = held.tile([P, count * C], U8, name=f"slot_scales{first}", align_bytes=64)
+            else:
+                codes = place([P, C], U32, f"slot_codes{first}", 2 * (first - AHEAD))
+                scales = place([P, C], U8, f"slot_scales{first}", 2 * (first - AHEAD) + 1)
             nc.vector.tensor_copy(codes[:], x_codes[:].indirect(entries))
             nc.vector.tensor_copy(scales[:], x_scales[:].indirect(entries))
-            for q in range(HALF):
-                slots_mx[HALF * half + q] = (codes[:, q * C : (q + 1) * C], scales[:, q * C : (q + 1) * C])
+            for q in range(count):
+                slots_mx[first + q] = (codes[:, q * C : (q + 1) * C], scales[:, q * C : (q + 1) * C])
 
-        def round_w13(kind, e, engines):
-            if kind == "w3":
-                w13_rounded[e] = rounded.tile([P, 2, H * PACK], BF16, name="w_rounded", align_bytes=64)
+        w13_rounded = place([P, 3 * WIDE], BF16, "w13_rounded", ROUNDED_ROOM)
+
+        def places(e):
+            return {"w1": 2 * (e % 2), "w3": 1}
+
+        def round_w13(kind, e, shares):
             src = raws[kind, e][:].rearrange("p j (m t) -> p m j t", t=PACK)
-            dst = w13_rounded[e][:, 0 if kind == "w1" else 1, :].rearrange("p (t m j) -> p m j t", t=PACK, j=PACK)
-            for part, engine in enumerate(engines):
-                ms = slice(part * P // len(engines), (part + 1) * P // len(engines))
-                if engine == "vector":
-                    nc.vector.tensor_copy(out=dst[:, ms], in_=src[:, ms])
-                else:
-                    nc.scalar.copy(out=dst[:, ms], in_=src[:, ms])
+            dst = w13_rounded[:, places(e)[kind] * WIDE : (places(e)[kind] + 1) * WIDE].rearrange("p (t m j) -> p m j t", t=PACK, j=PACK)
+            for engine, ms in shares:
+                copy_on(engine, dst[:, ms], src[:, ms])
 
-        def allocate_w13(e):
-            codes = quantised.tile([P, 2 * H], U32, name="w13_codes", align_bytes=64)
-            scales = quantised.tile([P, 2 * H], U8, name="w13_scales", align_bytes=64)
+        def quantize_w13(e):
+            codes = work.tile([P, 2 * H], U32, name="w13_codes", align_bytes=64)
+            scales = work.tile([P, 2 * H], U8, name="w13_scales", align_bytes=64)
+            quantize(codes[:], scales[:], w13_rounded[:, e % 2 * WIDE : (e % 2 + 2) * WIDE])
             w13_mx[e] = (codes, scales)
-            return codes, scales
 
-        def first_layer(e):
-            if e in (OWN_HOST, LAST):
-                host = raws["w1", e][:, 2:4, :]
-            else:
-                host = raws["w1", e + 1][:, 0:2, :]
-            if e == LAST:
-                h = held.tile([P, C, PACK], BF16, name="last_h", tag="middle", align_bytes=64)
-            else:
-                h = work.tile([P, C, PACK], BF16, name="h", align_bytes=64)
+        def first_products(e):
             w_codes, w_scales = w13_mx[e]
             slot_codes, slot_scales = slots_mx[e]
             for s in range(C // P):
                 slots = slice(s * P, (s + 1) * P)
-                sums = []
-                for k, (kind, banks) in enumerate((("w1", banks_a), ("w3", banks_g))):
+                for kind, banks in (("w1", banks_a), ("w3", banks_g)):
+                    k = places(e)[kind] - e % 2
                     acc = banks.tile([P, PACK, P], F32, name=f"acc_{kind}")
                     for t in range(PACK):
                         cols = slice(k * H + t * P, k * H + (t + 1) * P)
@@ -195,167 +191,163 @@ def tile_moe_tk_glu_sigmoid_kernel(
                             (w_codes[:, cols], w_scales[:, cols]),
                             (slot_codes[:, slots], slot_scales[:, slots]),
                         )
-                    sums.append(acc[:].rearrange("p t (c i) -> p c t i", i=2))
-                sig = host[:, s, :].rearrange("p (c t i) -> p c t i", t=PACK, i=2)
-                nc.scalar.activation(sig, sums[0], SIGMOID)
-                nc.vector.tensor_tensor(h[:, slots, :].rearrange("p (c i) t -> p c t i", i=2), sig, sums[1], MULT)
-            h_rounded[e] = h
+                    sums[e, s, kind] = acc[:].rearrange("p t (c i) -> p c t i", i=2)
 
-        def quantize_h(e):
-            codes = held.tile([P, C], U32, name=f"h_codes{e}", align_bytes=64)
-            scales = held.tile([P, C], U8, name=f"h_scales{e}", align_bytes=64)
-            quantize(codes[:], scales[:], h_rounded[e][:].rearrange("p s t -> p (s t)"))
-            h_mx[e] = (codes, scales)
-
-        def round_w2(c, half, pieces_on_vector):
-            if half == 1 and c > 0:
-                values = held.tile([P, H * PACK], BF16, name="late_w2", tag=f"late{c}", align_bytes=64)
-            elif c == 1:
-                values = single.tile([P, H * PACK], BF16, name="first_products", align_bytes=64)
-            elif half == 0:
-                values = held.tile([P, H * PACK], BF16, name="middle_w2", tag="middle", align_bytes=64)
-            else:
-                values = rounded.tile([P, H * PACK], BF16, name="w_rounded", align_bytes=64)
-            for q in range(HALF):
-                interleave(
-                    q >= HALF - pieces_on_vector,
-                    values[:, q * P * PACK : (q + 1) * P * PACK],
-                    raws[c, half][:, q, :].rearrange("p (j n) -> p j n", j=PACK),
+        def gated_units(e):
+            if e % 2 == 0:
+                h_rounded[e // 2] = work.tile([P, 2 * C, PACK], BF16, name="h", align_bytes=64)
+            h = h_rounded[e // 2][:, e % 2 * C : (e % 2 + 1) * C, :]
+            for s in range(C // P):
+                slots = slice(s * P, (s + 1) * P)
+                if e == LAST:
+                    host = held.tile([P, PACK * P], F32, name="sig", tag=f"last_sig{s}", align_bytes=64)[:]
+                elif e + AHEAD < E:
+                    host = place([P, PACK * P], F32, f"sig{e}_{s}", 2 * e + s)[:]
+                else:
+                    host = raws["w3" if s == 1 and e + 1 < LAST else "w1", e + 1][:, 2 + s, :]
+                sig = host.rearrange("p (c t i) -> p c t i", t=PACK, i=2)
+                nc.scalar.activation(sig, sums[e, s, "w1"], SIGMOID)
+                nc.vector.tensor_tensor(
+                    h[:, slots, :].rearrange("p (c i) t -> p c t i", i=2), sig, sums[e, s, "w3"], MULT
                 )
-            w2_rounded[c, half] = values
 
-        def quantize_w2(c, half):
-            if (c, half) == (0, 1):
-                codes = held.tile([P, HALF * P], U32, name="late_codes", tag="late1", align_bytes=64)
-            elif (c, half) == (CHUNKS - 1, 1):
-                codes = held.tile([P, HALF * P], U32, name="last_codes", tag="apart", align_bytes=64)
+        def quantize_h(first, count):
+            codes = held.tile([P, count * C], U32, name=f"h_codes{first}", align_bytes=64)
+            scales = held.tile([P, count * C], U8, name=f"h_scales{first}", align_bytes=64)
+            values = h_rounded[first // 2][:, first % 2 * C : (first % 2 + count) * C, :]
+            quantize(codes[:], scales[:], values.rearrange("p s t -> p (s t)"))
+            for q in range(count):
+                h_mx[first + q] = (codes[:, q * C : (q + 1) * C], scales[:, q * C : (q + 1) * C])
+
+        def round_w2(c, half):
+            if c == 0:
+                values = w13_rounded[:, half * WIDE : (half + 1) * WIDE]
             else:
-                codes = quantised.tile([P, HALF * P], U32, name="w2_codes", align_bytes=64)
-            scales = quantised.tile([P, HALF * P], U8, name="w2_scales", align_bytes=64)
+                tag = {(1, 0): "last_sig0", (1, 1): "codes0", (2, 0): "codes1", (2, 1): "scales1"}[c, half]
+                values = held.tile([P, HALF * P * PACK], BF16, name="w2_rounded", tag=tag, align_bytes=64)
+            pairs = [values[:, part * 2 * P * PACK : (part + 1) * 2 * P * PACK] for part in range(2)]
+            if (c, half) == (0, 1):
+                last_pair = held.tile([P, 2 * P * PACK], BF16, name="last_pair", tag="last_sig0", align_bytes=64)
+                pairs[1] = last_pair[:]
+            for part in range(2):
+                copy_on(
+                    "vector" if 2 * half + part in PAIRS_ON_VECTOR[c] else "scalar",
+                    pairs[part].rearrange("p (q c i j) -> p q c j i", q=2, i=PACK, j=PACK),
+                    raws[c, half][:, 2 * part : 2 * part + 2, :].rearrange("p q (j c i) -> p q c j i", i=PACK, j=PACK),
+                )
+            w2_rounded[c, half] = pairs if half == 1 else [values[:, :]]
+
+        def second_layer(c, half):
+            tags = (f"codes{c}", f"scales{c}") if half == 1 else ("first_codes", "first_scales")
+            codes = held.tile([P, HALF * P], U32, name="w2_codes", tag=tags[0], align_bytes=64)
+            scales = held.tile([P, HALF * P], U8, name="w2_scales", tag=tags[1], align_bytes=64)
             parts = 1 + half
             for part in range(parts):
                 words = slice(part * HALF * P // parts, (part + 1) * HALF * P // parts)
-                values = w2_rounded[c, half][:, words.start * PACK : words.stop * PACK]
+                values = w2_rounded[c, half][part]
                 quantize(codes[:, words], scales[:, words], values)
-            w2_mx[c, half] = (codes, scales)
-
-        def second_layer(c, half):
-            codes, scales = w2_mx[c, half]
+            w2_mx[c, half] = codes
             for pair in range(HALF // 2):
                 acc = banks_y.tile([P, 2 * C], F32, name="acc_y")
                 first = HALF * half + 2 * pair
                 for q in range(2):
                     cols = slice((2 * pair + q) * P, (2 * pair + q + 1) * P)
                     h_codes, h_scales = h_mx[first + q]
-                    multiply(acc[:, q * C : (q + 1) * C], (codes[:, cols], scales[:, cols]), (h_codes[:], h_scales[:]))
+                    multiply(acc[:, q * C : (q + 1) * C], (codes[:, cols], scales[:, cols]), (h_codes, h_scales))
                 nc.scalar.copy(out=y_rows[c][:, first * C : (first + 2) * C], in_=acc[:])
 
         def gather_results(c):
-            if c == 0:
-                early = single.tile([P, R, T], F32, name="first_products", align_bytes=64)
-                late = held.tile([P, 2, T], F32, name="late_products", tag="late1", align_bytes=64)
-                terms = [early[:, 0, :], early[:, 1, :], late[:, 0, :], late[:, 1, :]]
-            elif c == 1:
-                early = ring.tile([P, PACK, H], F32, name="raw", align_bytes=64)
-                late = held.tile([P, 2, T], F32, name="late_products", tag="late2", align_bytes=64)
-                middle = held.tile([P, 2, T], F32, name="middle_products", tag="middle", align_bytes=64)
-                terms = [early[:, 0, :], middle[:, 0, :], middle[:, 1, :], late[:, 0, :]]
+            early = work.tile([P, 2, T], F32, name="early_products", align_bytes=64)
+            late = held.tile([P, 2, T], F32, name="late_products", tag=("codes0", "scales1", "codes1")[c], align_bytes=64)
+            products[c] = [early[:, 0, :], early[:, 1, :], late[:, 0, :], late[:, 1, :]]
+            if c < CHUNKS - 1:
+                order = [(r, slice(0, T)) for r in range(R)]
             else:
-                early = single.tile([P, R, T], F32, name="first_products", align_bytes=64)
-                terms = [early[:, r, :] for r in range(R)]
-            for r in range(R):
-                nc.vector.tensor_tensor(terms[r], y_rows[c][:].indirect(pos_t[r][:]), gates[:, r, :], MULT)
-            products[c] = terms
+                first, second = token_halves
+                order = [(0, second), (1, second), (0, first), (1, first), (2, first), (2, second), (3, first), (3, second)]
+            for r, tokens in order:
+                entries = pos_t[r][:, tokens.start // LIST_ROWS : tokens.stop // LIST_ROWS]
+                nc.vector.tensor_tensor(products[c][r][:, tokens], y_rows[c][:].indirect(entries), gates[:, r, tokens], MULT)
 
-        blocks = [slice(b * P, (b + 1) * P) for b in range(T // P)]
+        def blocks(tokens):
+            return [slice(b, b + P) for b in range(0, tokens.stop - tokens.start, P)]
 
-        def add_turned(c, count):
-            acc = banks_g.tile([P, T], F32, name="acc_w3")
+        def add_turned(c, tokens, count):
+            acc = banks_g.tile([P, tokens.stop - tokens.start], F32, name="acc_w3")
             for r in range(count):
-                for cols in blocks:
+                for cols in blocks(tokens):
                     nc.tensor.matmul(
                         acc[:, cols],
-                        lhsT=products[c][r][:, cols],
+                        lhsT=products[c][r][:, tokens][:, cols],
                         rhs=ident[:],
                         start=r == 0 and cols.start == 0,
-                        stop=r == count - 1 and cols.stop == T,
+                        stop=r == count - 1 and cols.stop == tokens.stop - tokens.start,
                         is_transpose=True,
                     )
-            turned[c] = acc
+            turned[c, tokens.start] = acc
 
-        def turn_back(c):
-            if c == 0:
-                staged = held.tile([P, T], F32, name="staged_late", tag="apart", align_bytes=64)
-            else:
-                staged = work.tile([P, T], F32, name="staged")
-            nc.scalar.copy(out=staged[:], in_=turned[c][:])
-            back = banks_a.tile([P, T], F32, name="acc_w1")
-            for cols in blocks:
+        def turn_back(c, tokens, tag):
+            staged = held.tile([P, tokens.stop - tokens.start], F32, name="staged", tag=tag, align_bytes=64)
+            nc.scalar.copy(out=staged[:], in_=turned[c, tokens.start][:])
+            back = banks_a.tile([P, tokens.stop - tokens.start], F32, name="acc_w1")
+            for cols in blocks(tokens):
                 nc.tensor.transpose(back[:, cols], staged[:, cols], ident[:])
             return back
 
-        def store_chunk(c):
-            back = turn_back(c)
+        def store_chunk(c, tag):
+            back = turn_back(c, slice(0, T), tag)
             result = work.tile([P, T], F32, name="result")
             nc.scalar.copy(out=result[:], in_=back[:])
             nc.sync.dma_start(out=out[c * P : (c + 1) * P, :], in_=result[:])
 
         def store_last_chunk():
             c = CHUNKS - 1
-            back = turn_back(c)
-            result = work.tile([P, T], F32, name="result")
+            first, second = token_halves
             terms = products[c]
-            nc.vector.tensor_tensor(terms[2], terms[2], terms[3], ADD)
-            for tokens in token_halves:
-                nc.vector.tensor_tensor(result[:, tokens], terms[2][:, tokens], back[:, tokens], ADD)
+            result = work.tile([P, T], F32, name="result")
+            add_turned(c, second, 2)
+            back = turn_back(c, second, "staged_second")
+            nc.vector.tensor_tensor(terms[2][:, second], terms[2][:, second], back[:], ADD)
+            add_turned(c, first, 3)
+            back = turn_back(c, first, "staged_first")
+            for tokens, partial in ((first, back[:]), (second, terms[2][:, second])):
+                nc.vector.tensor_tensor(result[:, tokens], terms[3][:, tokens], partial, ADD)
                 nc.sync.dma_start(out=out[c * P : (c + 1) * P, tokens], in_=result[:, tokens])
 
-        for half in range(2):
-            gather_tokens(half)
+        gather_tokens(0, HALF)
+        gather_tokens(HALF, AHEAD - HALF)
 
+        everything = slice(0, P)
         for e in range(E):
-            round_w13("w3", e, ("scalar",) if e < W3_ON_SCALAR else ("vector",))
-            load_next()
-            round_w13("w1", e, ("vector", "scalar") if e >= E - W1_SHARED else ("scalar",))
-            load_next()
-            if e >= 2:
-                quantize_h(e - 2)
-            codes, scales = allocate_w13(e)
-            if e < LAST:
-                quantize(codes[:], scales[:], w13_rounded[e][:].rearrange("p k c -> p (k c)"))
-                if e >= 1:
-                    first_layer(e - 1)
-            else:
-                quantize(codes[:, :H], scales[:, :H], w13_rounded[e][:, 0, :])
-                first_layer(e - 1)
-                quantize_h(e - 1)
-                quantize(codes[:, H:], scales[:, H:], w13_rounded[e][:, 1, :])
+            round_w13("w1", e, [("scalar", everything)])
+            shares = [("vector", slice(0, W3_ON_VECTOR[e])), ("scalar", slice(W3_ON_VECTOR[e], P))]
+            round_w13("w3", e, [share for share in shares if share[1].stop > share[1].start])
+            if e >= 3 and e % 2 == 1:
+                quantize_h(e - 3, 2)
+            quantize_w13(e)
+            if e >= 1:
+                gated_units(e - 1)
+            first_products(e)
+            if e == 0:
+                load_expert(LAST - 1)
+                load_expert(LAST)
+            if AHEAD <= e < AHEAD + CHUNKS:
+                for half in range(2):
+                    load_half(e - AHEAD, half)
+            if e >= 1 and e - 1 + AHEAD < E:
+                gather_tokens(e - 1 + AHEAD, 1)
+        quantize_h(LAST - 1, 1)
+        gated_units(LAST)
+        quantize_h(LAST, 1)
 
-        round_w2(0, 0, 0)
-        quantize_w2(0, 0)
-        first_layer(LAST)
-        round_w2(0, 1, 0)
-        quantize_h(LAST)
-        quantize_w2(0, 1)
-        second_layer(0, 0)
-        second_layer(0, 1)
-
-        for half in range(2):
-            round_w2(1, half, HALF if half == 0 else 0)
-            quantize_w2(1, half)
-            second_layer(1, half)
-        gather_results(0)
-        add_turned(0, R)
-
-        for half in range(2):
-            round_w2(2, half, LAST_PIECES_ON_VECTOR if half == 1 else 0)
-            quantize_w2(2, half)
-            second_layer(2, half)
-        gather_results(1)
-        add_turned(1, R)
-        store_chunk(0)
-        store_chunk(1)
-
-        gather_results(2)
-        add_turned(2, 2)
+        for c in range(CHUNKS):
+            for half in range(2):
+                round_w2(c, half)
+                second_layer(c, half)
+            if c >= 1:
+                gather_results(c - 1)
+                add_turned(c - 1, slice(0, T), R)
+        for c in range(CHUNKS - 1):
+            store_chunk(c, ("codes2", "scales2")[c])
+        gather_results(CHUNKS - 1)
         store_last_chunk()

@@ -26,11 +26,12 @@ HALF = E // 2
 LAST = E - 1
 WIDE = H * PACK
 ROOM = 4 * PACK * H
-RING = 7
+RING = 10
 AHEAD = 5
 WINDOW = 1408
-ROUNDED_ROOM = 2 * (E - AHEAD)
-W3_ON_VECTOR = (0, 64, 64, 64, 112, 112, 112, 128)
+ROUNDED_ROOM = E - AHEAD
+W3_ON_VECTOR = (0, 80, 80, 80, 104, 104, 104, 128)
+W3_ON_GPSIMD = (64, 48, 48, 48, 24, 24, 24, 0)
 PAIRS_ON_VECTOR = ((3,), (0, 1), ())
 
 
@@ -73,18 +74,18 @@ def tile_moe_tk_glu_sigmoid_kernel(
 
         def load_expert(e):
             for kind, matrix in (("w1", w1), ("w3", w3)):
-                if 1 <= e <= E - AHEAD:
-                    raw = place([P, PACK, H], F32, f"{kind}_{e}", 2 * (e - 1) + (kind == "w3"))
+                if 1 <= e <= E - AHEAD and kind == "w1":
+                    raw = place([P, PACK, H], F32, f"{kind}_{e}", e - 1)
                 else:
                     raw = ring.tile([P, PACK, H], F32, name="raw", align_bytes=64)
                 nc.sync.dma_start(out=raw[:], in_=matrix[e, :, :].rearrange("(p j) h -> p j h", j=PACK))
                 raws[kind, e] = raw
 
         def load_half(c, half):
-            if c == 0:
+            if c == 0 or half == 0:
                 raw = ring.tile([P, PACK, H], F32, name="raw", align_bytes=64)
             else:
-                raw = place([P, PACK, H], F32, f"w2_{c}_{half}", 2 * (c - 1) + half)
+                raw = place([P, PACK, H], F32, f"w2_{c}_{half}", c - 1)
             for q in range(HALF):
                 e = HALF * half + q
                 nc.sync.dma_start(out=raw[:, q, :].rearrange("p (j n) -> p j n", j=PACK), in_=w2[e, :, c * P : (c + 1) * P].rearrange("(p j) n -> p j n", j=PACK))
@@ -112,6 +113,9 @@ def tile_moe_tk_glu_sigmoid_kernel(
         def copy_on(engine, dst, src):
             if engine == "vector":
                 nc.vector.tensor_copy(out=dst, in_=src)
+            elif engine == "gpsimd":
+                order = "p m j t -> p t m j"
+                nc.gpsimd.tensor_scalar(dst.rearrange(order), src.rearrange(order), 1.0, 0.0, MULT, ADD)
             else:
                 nc.scalar.copy(out=dst, in_=src)
 
@@ -152,8 +156,8 @@ def tile_moe_tk_glu_sigmoid_kernel(
                 codes = held.tile([P, count * C], U32, name=f"slot_codes{first}", align_bytes=64)
                 scales = held.tile([P, count * C], U8, name=f"slot_scales{first}", align_bytes=64)
             else:
-                codes = place([P, C], U32, f"slot_codes{first}", 2 * (first - AHEAD))
-                scales = place([P, C], U8, f"slot_scales{first}", 2 * (first - AHEAD) + 1)
+                codes = place([P, C], U32, f"slot_codes{first}", first - AHEAD)
+                scales = place([P, C], U8, f"slot_scales{first}", first - AHEAD, ROOM // 4)
             nc.vector.tensor_copy(codes[:], x_codes[:].indirect(entries))
             nc.vector.tensor_copy(scales[:], x_scales[:].indirect(entries))
             for q in range(count):
@@ -202,9 +206,9 @@ def tile_moe_tk_glu_sigmoid_kernel(
                 if e == LAST:
                     host = held.tile([P, PACK * P], F32, name="sig", tag=f"last_sig{s}", align_bytes=64)[:]
                 elif e + AHEAD < E:
-                    host = place([P, PACK * P], F32, f"sig{e}_{s}", 2 * e + s)[:]
+                    host = place([P, PACK * P], F32, f"sig{e}_{s}", e, s * ROOM // 4)[:]
                 else:
-                    host = raws["w3" if s == 1 and e + 1 < LAST else "w1", e + 1][:, 2 + s, :]
+                    host = raws["w1", e + 1][:, 2 + s, :]
                 sig = host.rearrange("p (c t i) -> p c t i", t=PACK, i=2)
                 nc.scalar.activation(sig, sums[e, s, "w1"], SIGMOID)
                 nc.vector.tensor_tensor(
@@ -320,7 +324,8 @@ def tile_moe_tk_glu_sigmoid_kernel(
         everything = slice(0, P)
         for e in range(E):
             round_w13("w1", e, [("scalar", everything)])
-            shares = [("vector", slice(0, W3_ON_VECTOR[e])), ("scalar", slice(W3_ON_VECTOR[e], P))]
+            cut = W3_ON_VECTOR[e] + W3_ON_GPSIMD[e]
+            shares = [("vector", slice(0, W3_ON_VECTOR[e])), ("gpsimd", slice(W3_ON_VECTOR[e], cut)), ("scalar", slice(cut, P))]
             round_w13("w3", e, [share for share in shares if share[1].stop > share[1].start])
             if e >= 3 and e % 2 == 1:
                 quantize_h(e - 3, 2)

@@ -26,13 +26,14 @@ HALF = E // 2
 LAST = E - 1
 WIDE = H * PACK
 ROOM = 4 * PACK * H
-RING = 10
+ROOMS = 13
+QUARTER = ROOM // 4
 AHEAD = 5
 WINDOW = 1408
-ROUNDED_ROOM = E - AHEAD
-W3_ON_VECTOR = (0, 80, 80, 80, 104, 104, 104, 128)
-W3_ON_GPSIMD = (64, 48, 48, 48, 24, 24, 24, 0)
-PAIRS_ON_VECTOR = ((3,), (0, 1), ())
+ROUNDED_ROOM = ROOMS
+W3_ON_VECTOR = (0, 72, 72, 72, 72, 72, 72, 128)
+W3_ON_GPSIMD = (64, 40, 40, 40, 40, 40, 40, 0)
+PAIR_ENGINES = (("scalar", "vector", "gpsimd", "scalar"), ("vector", "vector", "scalar", "scalar"), ("scalar",) * 4)
 
 
 def tile_moe_tk_glu_sigmoid_kernel(
@@ -41,7 +42,6 @@ def tile_moe_tk_glu_sigmoid_kernel(
     nc = tc.nc
     with ExitStack() as ctx:
         held = ctx.enter_context(tc.tile_pool(name="held", bufs=1))
-        ring = ctx.enter_context(tc.tile_pool(name="ring", bufs=RING))
         placed = ctx.enter_context(tc.tile_pool(name="placed", bufs=1))
         work = ctx.enter_context(tc.tile_pool(name="work", bufs=2))
         banks_a = ctx.enter_context(tc.psum_pool(name="banks_a", bufs=3))
@@ -64,7 +64,7 @@ def tile_moe_tk_glu_sigmoid_kernel(
         token_halves = [slice(half * (T // 2), (half + 1) * (T // 2)) for half in range(2)]
         x_raw = []
         for half, tokens in enumerate(token_halves):
-            raw_half = held.tile([P, PACK, T // 2], F32, name="x_raw", tag=("codes0", "scales1")[half], align_bytes=64)
+            raw_half = held.tile([P, PACK, T // 2], F32, name="x_raw", tag=f"last_sig{half}", align_bytes=64)
             nc.sync.dma_start(out=raw_half[:], in_=xT[:, tokens].rearrange("(p j) t -> p j t", j=PACK))
             x_raw.append(raw_half)
         offs_t = held.tile([P, S // LIST_ROWS], U16, name="offs_t")
@@ -72,24 +72,21 @@ def tile_moe_tk_glu_sigmoid_kernel(
 
         raws = {}
 
+        def room_of(kind, e):
+            n = 2 * e + (kind == "w3")
+            return n if n < ROOMS else {13: 0, 14: 1, 15: 3}[n]
+
         def load_expert(e):
             for kind, matrix in (("w1", w1), ("w3", w3)):
-                if 1 <= e <= E - AHEAD and kind == "w1":
-                    raw = place([P, PACK, H], F32, f"{kind}_{e}", e - 1)
-                else:
-                    raw = ring.tile([P, PACK, H], F32, name="raw", align_bytes=64)
+                raw = place([P, PACK, H], F32, f"{kind}_{e}", room_of(kind, e))
                 nc.sync.dma_start(out=raw[:], in_=matrix[e, :, :].rearrange("(p j) h -> p j h", j=PACK))
                 raws[kind, e] = raw
 
         def load_half(c, half):
-            if c == 0 or half == 0:
-                raw = ring.tile([P, PACK, H], F32, name="raw", align_bytes=64)
-            else:
-                raw = place([P, PACK, H], F32, f"w2_{c}_{half}", c - 1)
+            raw = place([P, HALF, PACK, P], F32, f"w2_{c}_{half}", (5, 7, 9, 11, 2, 6)[2 * c + half])
             for q in range(HALF):
-                e = HALF * half + q
-                nc.sync.dma_start(out=raw[:, q, :].rearrange("p (j n) -> p j n", j=PACK), in_=w2[e, :, c * P : (c + 1) * P].rearrange("(p j) n -> p j n", j=PACK))
-
+                columns = w2[HALF * half + q, :, c * P : (c + 1) * P]
+                nc.sync.dma_start(out=raw[:, q], in_=columns.rearrange("(p j) n -> p j n", j=PACK))
             raws[c, half] = raw
 
         for e in range(E - 2):
@@ -140,7 +137,7 @@ def tile_moe_tk_glu_sigmoid_kernel(
                 stop=True,
             )
 
-        x_rounded = held.tile([P, T * PACK], BF16, name="x_rounded", tag="codes1", align_bytes=64)
+        x_rounded = held.tile([P, T * PACK], BF16, name="x_rounded", align_bytes=64)
         for half, tokens in enumerate(token_halves):
             values = x_rounded[:, tokens.start * PACK : tokens.stop * PACK]
             interleave("vector", values, x_raw[half][:])
@@ -150,18 +147,17 @@ def tile_moe_tk_glu_sigmoid_kernel(
         slots_mx, w13_mx, sums, h_rounded, h_mx = {}, {}, {}, {}, {}
         w2_rounded, w2_mx, products, turned = {}, {}, {}, {}
 
-        def gather_tokens(first, count):
+        def gather_tokens(sort, first, count, step):
             entries = offs_t[:, first * (C // LIST_ROWS) : (first + count) * (C // LIST_ROWS)]
-            if first < AHEAD:
-                codes = held.tile([P, count * C], U32, name=f"slot_codes{first}", align_bytes=64)
-                scales = held.tile([P, count * C], U8, name=f"slot_scales{first}", align_bytes=64)
+            window, dtype = ((x_codes, U32), (x_scales, U8))[sort]
+            name = f"slots{sort}_{first}"
+            if step == 0:
+                picked = held.tile([P, count * C], dtype, name=name, align_bytes=64)
             else:
-                codes = place([P, C], U32, f"slot_codes{first}", first - AHEAD)
-                scales = place([P, C], U8, f"slot_scales{first}", first - AHEAD, ROOM // 4)
-            nc.vector.tensor_copy(codes[:], x_codes[:].indirect(entries))
-            nc.vector.tensor_copy(scales[:], x_scales[:].indirect(entries))
+                picked = place([P, count * C], dtype, name, room_of("w1", step))
+            nc.vector.tensor_copy(picked[:], window[:].indirect(entries))
             for q in range(count):
-                slots_mx[first + q] = (codes[:, q * C : (q + 1) * C], scales[:, q * C : (q + 1) * C])
+                slots_mx[sort, first + q] = picked[:, q * C : (q + 1) * C]
 
         w13_rounded = place([P, 3 * WIDE], BF16, "w13_rounded", ROUNDED_ROOM)
 
@@ -175,95 +171,118 @@ def tile_moe_tk_glu_sigmoid_kernel(
                 copy_on(engine, dst[:, ms], src[:, ms])
 
         def quantize_w13(e):
-            codes = work.tile([P, 2 * H], U32, name="w13_codes", align_bytes=64)
-            scales = work.tile([P, 2 * H], U8, name="w13_scales", align_bytes=64)
-            quantize(codes[:], scales[:], w13_rounded[:, e % 2 * WIDE : (e % 2 + 2) * WIDE])
-            w13_mx[e] = (codes, scales)
+            if e < LAST:
+                codes = work.tile([P, 2 * H], U32, name="w13_codes", align_bytes=64)
+                scales = work.tile([P, 2 * H], U8, name="w13_scales", align_bytes=64)
+                quantize(codes[:], scales[:], w13_rounded[:, e % 2 * WIDE : (e % 2 + 2) * WIDE])
+                for kind in ("w1", "w3"):
+                    k = places(e)[kind] - e % 2
+                    w13_mx[kind, e] = (codes[:, k * H : (k + 1) * H], scales[:, k * H : (k + 1) * H])
+                return
+            for k, kind in enumerate(("w1", "w3")):
+                codes = place([P, H], U32, f"last_codes_{kind}", room_of("w1", LAST) - 1 + k)
+                scales = held.tile([P, H], U8, name=f"last_scales_{kind}", align_bytes=64)
+                start = places(e)[kind] * WIDE
+                quantize(codes[:], scales[:], w13_rounded[:, start : start + WIDE])
+                w13_mx[kind, e] = (codes[:], scales[:])
 
         def first_products(e):
-            w_codes, w_scales = w13_mx[e]
-            slot_codes, slot_scales = slots_mx[e]
-            for s in range(C // P):
+            slot_codes, slot_scales = slots_mx[0, e], slots_mx[1, e]
+            order = [(s, kind) for s in range(C // P) for kind in ("w1", "w3")]
+            if e == LAST:
+                order = [(s, kind) for kind in ("w1", "w3") for s in range(C // P)]
+            for s, kind in order:
                 slots = slice(s * P, (s + 1) * P)
-                for kind, banks in (("w1", banks_a), ("w3", banks_g)):
-                    k = places(e)[kind] - e % 2
-                    acc = banks.tile([P, PACK, P], F32, name=f"acc_{kind}")
-                    for t in range(PACK):
-                        cols = slice(k * H + t * P, k * H + (t + 1) * P)
-                        multiply(
-                            acc[:, t, :],
-                            (w_codes[:, cols], w_scales[:, cols]),
-                            (slot_codes[:, slots], slot_scales[:, slots]),
-                        )
-                    sums[e, s, kind] = acc[:].rearrange("p t (c i) -> p c t i", i=2)
+                w_codes, w_scales = w13_mx[kind, e]
+                acc = (banks_a if kind == "w1" else banks_g).tile([P, PACK, P], F32, name=f"acc_{kind}")
+                for t in range(PACK):
+                    cols = slice(t * P, (t + 1) * P)
+                    multiply(
+                        acc[:, t, :],
+                        (w_codes[:, cols], w_scales[:, cols]),
+                        (slot_codes[:, slots], slot_scales[:, slots]),
+                    )
+                sums[e, s, kind] = acc[:].rearrange("p t (c i) -> p c t i", i=2)
 
         def gated_units(e):
-            if e % 2 == 0:
-                h_rounded[e // 2] = work.tile([P, 2 * C, PACK], BF16, name="h", align_bytes=64)
-            h = h_rounded[e // 2][:, e % 2 * C : (e % 2 + 1) * C, :]
+            h = work.tile([P, C, PACK], BF16, name="h", align_bytes=64)
+            h_rounded[e] = h
             for s in range(C // P):
                 slots = slice(s * P, (s + 1) * P)
                 if e == LAST:
-                    host = held.tile([P, PACK * P], F32, name="sig", tag=f"last_sig{s}", align_bytes=64)[:]
-                elif e + AHEAD < E:
-                    host = place([P, PACK * P], F32, f"sig{e}_{s}", e, s * ROOM // 4)[:]
+                    host = place([P, PACK * P], F32, f"sig{e}_{s}", 4, s * QUARTER)
+                elif e == LAST - 1:
+                    host = place([P, PACK * P], F32, f"sig{e}_{s}", room_of("w1", LAST), (2 + s) * QUARTER)
                 else:
-                    host = raws["w1", e + 1][:, 2 + s, :]
-                sig = host.rearrange("p (c t i) -> p c t i", t=PACK, i=2)
+                    host = place([P, PACK * P], F32, f"sig{e}_{s}", room_of("w1", e + 1), s * QUARTER)
+                sig = host[:].rearrange("p (c t i) -> p c t i", t=PACK, i=2)
                 nc.scalar.activation(sig, sums[e, s, "w1"], SIGMOID)
                 nc.vector.tensor_tensor(
                     h[:, slots, :].rearrange("p (c i) t -> p c t i", i=2), sig, sums[e, s, "w3"], MULT
                 )
 
-        def quantize_h(first, count):
-            codes = held.tile([P, count * C], U32, name=f"h_codes{first}", align_bytes=64)
-            scales = held.tile([P, count * C], U8, name=f"h_scales{first}", align_bytes=64)
-            values = h_rounded[first // 2][:, first % 2 * C : (first % 2 + count) * C, :]
-            quantize(codes[:], scales[:], values.rearrange("p s t -> p (s t)"))
-            for q in range(count):
-                h_mx[first + q] = (codes[:, q * C : (q + 1) * C], scales[:, q * C : (q + 1) * C])
+        def quantize_h(e):
+            codes = held.tile([P, C], U32, name=f"h_codes{e}", align_bytes=64)
+            scales = held.tile([P, C], U8, name=f"h_scales{e}", align_bytes=64)
+            quantize(codes[:], scales[:], h_rounded[e][:].rearrange("p s t -> p (s t)"))
+            h_mx[e] = (codes[:], scales[:])
 
         def round_w2(c, half):
+            width = 2 * P * PACK
             if c == 0:
-                values = w13_rounded[:, half * WIDE : (half + 1) * WIDE]
+                starts = ((0, WIDE + width), (WIDE, 2 * WIDE))[half]
+                pairs = [w13_rounded[:, start : start + width] for start in starts]
+            elif half == 0:
+                values = place([P, WIDE], BF16, f"w2_rounded{c}", *((4, 0), (8, 0))[c - 1])
+                pairs = [values[:, part * width : (part + 1) * width] for part in range(2)]
             else:
-                tag = {(1, 0): "last_sig0", (1, 1): "codes0", (2, 0): "codes1", (2, 1): "scales1"}[c, half]
-                values = held.tile([P, HALF * P * PACK], BF16, name="w2_rounded", tag=tag, align_bytes=64)
-            pairs = [values[:, part * 2 * P * PACK : (part + 1) * 2 * P * PACK] for part in range(2)]
-            if (c, half) == (0, 1):
-                last_pair = held.tile([P, 2 * P * PACK], BF16, name="last_pair", tag="last_sig0", align_bytes=64)
-                pairs[1] = last_pair[:]
+                pairs = [place([P, width], BF16, f"w2_pair{c}_{part}", *pair_place(c, part))[:] for part in range(2)]
             for part in range(2):
-                copy_on(
-                    "vector" if 2 * half + part in PAIRS_ON_VECTOR[c] else "scalar",
-                    pairs[part].rearrange("p (q c i j) -> p q c j i", q=2, i=PACK, j=PACK),
-                    raws[c, half][:, 2 * part : 2 * part + 2, :].rearrange("p q (j c i) -> p q c j i", i=PACK, j=PACK),
-                )
-            w2_rounded[c, half] = pairs if half == 1 else [values[:, :]]
+                engine = PAIR_ENGINES[c][2 * half + part]
+                dst, src = pairs[part], raws[c, half][:, 2 * part : 2 * part + 2]
+                if engine == "gpsimd":
+                    for q in range(2):
+                        piece = dst[:, q * P * PACK : (q + 1) * P * PACK].rearrange("p (n j) -> p n j", j=PACK)
+                        nc.gpsimd.tensor_scalar(piece, src[:, q].rearrange("p j n -> p n j"), 1.0, 0.0, MULT, ADD)
+                else:
+                    copy_on(
+                        engine,
+                        dst.rearrange("p (q c i j) -> p q c j i", q=2, i=PACK, j=PACK),
+                        src.rearrange("p q j (c i) -> p q c j i", i=PACK),
+                    )
+            w2_rounded[c, half] = pairs if half == 1 or c == 0 else [values[:, :]]
+
+        def pair_place(c, part):
+            return (10, (1 + part) * QUARTER) if c == 1 else (8, (2 + part) * QUARTER)
 
         def second_layer(c, half):
-            tags = (f"codes{c}", f"scales{c}") if half == 1 else ("first_codes", "first_scales")
-            codes = held.tile([P, HALF * P], U32, name="w2_codes", tag=tags[0], align_bytes=64)
-            scales = held.tile([P, HALF * P], U8, name="w2_scales", tag=tags[1], align_bytes=64)
-            parts = 1 + half
+            rooms = {(0, 1): 10, (1, 0): 8, (1, 1): 11, (2, 0): 11, (2, 1): 6}
+            if (c, half) in rooms:
+                codes = place([P, HALF * P], U32, f"w2_codes{c}", rooms[c, half], (3 if c == 0 else 1) * QUARTER // 2)
+            else:
+                codes = held.tile([P, HALF * P], U32, name="w2_codes", tag=f"codes{min(c, 1)}", align_bytes=64)
+            if (c, half) == (1, 1):
+                scales = place([P, HALF * P], U8, "w2_scales", 8, 3 * QUARTER - 2 * P)
+            else:
+                scales = held.tile([P, HALF * P], U8, name=f"scales{half}", align_bytes=64)
+            parts = len(w2_rounded[c, half])
             for part in range(parts):
                 words = slice(part * HALF * P // parts, (part + 1) * HALF * P // parts)
-                values = w2_rounded[c, half][part]
-                quantize(codes[:, words], scales[:, words], values)
-            w2_mx[c, half] = codes
+                quantize(codes[:, words], scales[:, words], w2_rounded[c, half][part])
             for pair in range(HALF // 2):
                 acc = banks_y.tile([P, 2 * C], F32, name="acc_y")
                 first = HALF * half + 2 * pair
                 for q in range(2):
                     cols = slice((2 * pair + q) * P, (2 * pair + q + 1) * P)
-                    h_codes, h_scales = h_mx[first + q]
-                    multiply(acc[:, q * C : (q + 1) * C], (codes[:, cols], scales[:, cols]), (h_codes, h_scales))
+                    multiply(acc[:, q * C : (q + 1) * C], (codes[:, cols], scales[:, cols]), h_mx[first + q])
                 nc.scalar.copy(out=y_rows[c][:, first * C : (first + 2) * C], in_=acc[:])
 
         def gather_results(c):
             early = work.tile([P, 2, T], F32, name="early_products", align_bytes=64)
-            late = held.tile([P, 2, T], F32, name="late_products", tag=("codes0", "scales1", "codes1")[c], align_bytes=64)
-            products[c] = [early[:, 0, :], early[:, 1, :], late[:, 0, :], late[:, 1, :]]
+            products[c] = [early[:, r, :] for r in range(1 if c == 0 else 2)]
+            for r in range(len(products[c]), R):
+                where = ((10, (2 * r - 1) * QUARTER // 2), (8, r * QUARTER), (12, (r - 2) * QUARTER))[c]
+                products[c].append(place([P, T], F32, f"late_products{c}_{r}", *where)[:])
             if c < CHUNKS - 1:
                 order = [(r, slice(0, T)) for r in range(R)]
             else:
@@ -291,7 +310,7 @@ def tile_moe_tk_glu_sigmoid_kernel(
             turned[c, tokens.start] = acc
 
         def turn_back(c, tokens, tag):
-            staged = held.tile([P, tokens.stop - tokens.start], F32, name="staged", tag=tag, align_bytes=64)
+            staged = place([P, tokens.stop - tokens.start], F32, f"staged{c}_{tokens.start}", *tag)
             nc.scalar.copy(out=staged[:], in_=turned[c, tokens.start][:])
             back = banks_a.tile([P, tokens.stop - tokens.start], F32, name="acc_w1")
             for cols in blocks(tokens):
@@ -310,16 +329,17 @@ def tile_moe_tk_glu_sigmoid_kernel(
             terms = products[c]
             result = work.tile([P, T], F32, name="result")
             add_turned(c, second, 2)
-            back = turn_back(c, second, "staged_second")
+            back = turn_back(c, second, (12, 2 * QUARTER))
             nc.vector.tensor_tensor(terms[2][:, second], terms[2][:, second], back[:], ADD)
             add_turned(c, first, 3)
-            back = turn_back(c, first, "staged_first")
+            back = turn_back(c, first, (12, 3 * QUARTER))
             for tokens, partial in ((first, back[:]), (second, terms[2][:, second])):
                 nc.vector.tensor_tensor(result[:, tokens], terms[3][:, tokens], partial, ADD)
                 nc.sync.dma_start(out=out[c * P : (c + 1) * P, tokens], in_=result[:, tokens])
 
-        gather_tokens(0, HALF)
-        gather_tokens(HALF, AHEAD - HALF)
+        for first, count in ((0, HALF), (HALF, AHEAD - HALF)):
+            for sort in range(2):
+                gather_tokens(sort, first, count, 0)
 
         everything = slice(0, P)
         for e in range(E):
@@ -327,32 +347,33 @@ def tile_moe_tk_glu_sigmoid_kernel(
             cut = W3_ON_VECTOR[e] + W3_ON_GPSIMD[e]
             shares = [("vector", slice(0, W3_ON_VECTOR[e])), ("gpsimd", slice(W3_ON_VECTOR[e], cut)), ("scalar", slice(cut, P))]
             round_w13("w3", e, [share for share in shares if share[1].stop > share[1].start])
-            if e >= 3 and e % 2 == 1:
-                quantize_h(e - 3, 2)
+            if e >= 2:
+                quantize_h(e - 2)
             quantize_w13(e)
             if e >= 1:
                 gated_units(e - 1)
             first_products(e)
-            if e == 0:
-                load_expert(LAST - 1)
-                load_expert(LAST)
-            if AHEAD <= e < AHEAD + CHUNKS:
-                for half in range(2):
-                    load_half(e - AHEAD, half)
-            if e >= 1 and e - 1 + AHEAD < E:
-                gather_tokens(e - 1 + AHEAD, 1)
-        quantize_h(LAST - 1, 1)
+            if e < 2:
+                load_expert(LAST - 1 + e)
+            elif e < LAST:
+                load_half((e - 2) // 2, e % 2)
+            if e == LAST - 1:
+                load_half(CHUNKS - 1, 1)
+            if 1 <= e < LAST:
+                gather_tokens((e - 1) % 2, AHEAD + (e - 1) // 2, 1, e)
+        quantize_h(LAST - 1)
         gated_units(LAST)
-        quantize_h(LAST, 1)
+        quantize_h(LAST)
 
         for c in range(CHUNKS):
             for half in range(2):
                 round_w2(c, half)
+            for half in range(2):
                 second_layer(c, half)
             if c >= 1:
                 gather_results(c - 1)
                 add_turned(c - 1, slice(0, T), R)
         for c in range(CHUNKS - 1):
-            store_chunk(c, ("codes2", "scales2")[c])
+            store_chunk(c, (6, c * QUARTER))
         gather_results(CHUNKS - 1)
         store_last_chunk()

@@ -28,12 +28,12 @@ WIDE = H * PACK
 ROOM = 4 * PACK * H
 ROOMS = 13
 QUARTER = ROOM // 4
+W2_ROOMS = (5, 7, 9, 11, 2, 6)
 AHEAD = 5
 WINDOW = 1408
 ROUNDED_ROOM = ROOMS
-W3_ON_VECTOR = (0, 72, 72, 72, 72, 72, 72, 128)
-W3_ON_GPSIMD = (64, 40, 40, 40, 40, 40, 40, 0)
-PAIR_ENGINES = (("scalar", "vector", "gpsimd", "scalar"), ("vector", "vector", "scalar", "scalar"), ("scalar",) * 4)
+W3_ON_VECTOR = (0, 96, 96, 96, 96, 96, 96, 128)
+FIRST_HALF_ENGINE = ("scalar", "vector", "scalar")
 
 
 def tile_moe_tk_glu_sigmoid_kernel(
@@ -83,11 +83,14 @@ def tile_moe_tk_glu_sigmoid_kernel(
                 raws[kind, e] = raw
 
         def load_half(c, half):
-            raw = place([P, HALF, PACK, P], F32, f"w2_{c}_{half}", (5, 7, 9, 11, 2, 6)[2 * c + half])
-            for q in range(HALF):
-                columns = w2[HALF * half + q, :, c * P : (c + 1) * P]
-                nc.sync.dma_start(out=raw[:, q], in_=columns.rearrange("(p j) n -> p j n", j=PACK))
-            raws[c, half] = raw
+            room = W2_ROOMS[2 * c + half]
+            groups = ((0, 4),) if half == 0 else ((4, 2), (6, 2))
+            for first, count in groups:
+                raw = place([P, count, PACK, P], F32, f"w2_{c}_{first}", room, first % HALF * QUARTER)
+                for q in range(count):
+                    columns = w2[first + q, :, c * P : (c + 1) * P]
+                    nc.sync.dma_start(out=raw[:, q], in_=columns.rearrange("(p j) n -> p j n", j=PACK))
+                raws[c, first] = raw
 
         for e in range(E - 2):
             load_expert(e)
@@ -110,9 +113,6 @@ def tile_moe_tk_glu_sigmoid_kernel(
         def copy_on(engine, dst, src):
             if engine == "vector":
                 nc.vector.tensor_copy(out=dst, in_=src)
-            elif engine == "gpsimd":
-                order = "p m j t -> p t m j"
-                nc.gpsimd.tensor_scalar(dst.rearrange(order), src.rearrange(order), 1.0, 0.0, MULT, ADD)
             else:
                 nc.scalar.copy(out=dst, in_=src)
 
@@ -210,7 +210,7 @@ def tile_moe_tk_glu_sigmoid_kernel(
             for s in range(C // P):
                 slots = slice(s * P, (s + 1) * P)
                 if e == LAST:
-                    host = place([P, PACK * P], F32, f"sig{e}_{s}", 4, s * QUARTER)
+                    host = place([P, PACK * P], F32, f"sig{e}_{s}", W2_ROOMS[0], s * QUARTER)
                 elif e == LAST - 1:
                     host = place([P, PACK * P], F32, f"sig{e}_{s}", room_of("w1", LAST), (2 + s) * QUARTER)
                 else:
@@ -227,61 +227,65 @@ def tile_moe_tk_glu_sigmoid_kernel(
             quantize(codes[:], scales[:], h_rounded[e][:].rearrange("p s t -> p (s t)"))
             h_mx[e] = (codes[:], scales[:])
 
-        def round_w2(c, half):
-            width = 2 * P * PACK
-            if c == 0:
-                starts = ((0, WIDE + width), (WIDE, 2 * WIDE))[half]
-                pairs = [w13_rounded[:, start : start + width] for start in starts]
-            elif half == 0:
-                values = place([P, WIDE], BF16, f"w2_rounded{c}", *((4, 0), (8, 0))[c - 1])
-                pairs = [values[:, part * width : (part + 1) * width] for part in range(2)]
-            else:
-                pairs = [place([P, width], BF16, f"w2_pair{c}_{part}", *pair_place(c, part))[:] for part in range(2)]
+        def round_pieces(engine, dst, src):
+            copy_on(
+                engine,
+                dst.rearrange("p (q c i j) -> p q c j i", c=P // PACK, i=PACK, j=PACK),
+                src.rearrange("p q j (c i) -> p q c j i", i=PACK),
+            )
+
+        def round_first_half():
             for part in range(2):
-                engine = PAIR_ENGINES[c][2 * half + part]
-                dst, src = pairs[part], raws[c, half][:, 2 * part : 2 * part + 2]
-                if engine == "gpsimd":
-                    for q in range(2):
-                        piece = dst[:, q * P * PACK : (q + 1) * P * PACK].rearrange("p (n j) -> p n j", j=PACK)
-                        nc.gpsimd.tensor_scalar(piece, src[:, q].rearrange("p j n -> p n j"), 1.0, 0.0, MULT, ADD)
+                values = w13_rounded[:, part * WIDE // 2 : (part + 1) * WIDE // 2]
+                round_pieces("scalar", values, raws[0, 0][:, 2 * part : 2 * part + 2])
+
+        def round_w2(c):
+            width = 2 * P * PACK
+            room = W2_ROOMS[2 * c + 1]
+            if c == 0:
+                pairs = [w13_rounded[:, start : start + width] for start in (0, width, 2 * WIDE)]
+                w2_rounded[c] = [w13_rounded[:, 0:WIDE], pairs[2]]
+            else:
+                values = place([P, WIDE], BF16, f"w2_rounded{c}", *((W2_ROOMS[0], 0), (8, 0))[c - 1])
+                third = place([P, width], BF16, f"w2_third{c}", *((10, QUARTER), (8, 2 * QUARTER))[c - 1])
+                pairs = [values[:, 0:width], values[:, width:WIDE], third[:]]
+                w2_rounded[c] = [values[:], third[:]]
+            for part in range(2 if c > 0 else 0):
+                round_pieces(FIRST_HALF_ENGINE[c], pairs[part], raws[c, 0][:, 2 * part : 2 * part + 2])
+            round_pieces("scalar", pairs[2], raws[c, 4][:])
+            last = place([P, width], BF16, f"w2_last{c}", room)
+            round_pieces("vector", last[:], raws[c, 6][:])
+            w2_rounded[c].append(last[:])
+
+        def second_layer(c):
+            first_place = (None, (8, QUARTER // 2), (12, 0))[c]
+            last_place = ((10, QUARTER), (12, 0), (3, QUARTER - P * 4))[c]
+            scale_place = (None, (8, 2 * QUARTER), None)[c]
+            for part, (first, count) in enumerate(((0, 4), (4, 2), (6, 2))):
+                where = (first_place, None, last_place)[part]
+                if where is None:
+                    codes = held.tile([P, count * P], U32, name=f"codes{part}", align_bytes=64)
                 else:
-                    copy_on(
-                        engine,
-                        dst.rearrange("p (q c i j) -> p q c j i", q=2, i=PACK, j=PACK),
-                        src.rearrange("p q j (c i) -> p q c j i", i=PACK),
-                    )
-            w2_rounded[c, half] = pairs if half == 1 or c == 0 else [values[:, :]]
-
-        def pair_place(c, part):
-            return (10, (1 + part) * QUARTER) if c == 1 else (8, (2 + part) * QUARTER)
-
-        def second_layer(c, half):
-            rooms = {(0, 1): 10, (1, 0): 8, (1, 1): 11, (2, 0): 11, (2, 1): 6}
-            if (c, half) in rooms:
-                codes = place([P, HALF * P], U32, f"w2_codes{c}", rooms[c, half], (3 if c == 0 else 1) * QUARTER // 2)
-            else:
-                codes = held.tile([P, HALF * P], U32, name="w2_codes", tag=f"codes{min(c, 1)}", align_bytes=64)
-            if (c, half) == (1, 1):
-                scales = place([P, HALF * P], U8, "w2_scales", 8, 3 * QUARTER - 2 * P)
-            else:
-                scales = held.tile([P, HALF * P], U8, name=f"scales{half}", align_bytes=64)
-            parts = len(w2_rounded[c, half])
-            for part in range(parts):
-                words = slice(part * HALF * P // parts, (part + 1) * HALF * P // parts)
-                quantize(codes[:, words], scales[:, words], w2_rounded[c, half][part])
-            for pair in range(HALF // 2):
-                acc = banks_y.tile([P, 2 * C], F32, name="acc_y")
-                first = HALF * half + 2 * pair
-                for q in range(2):
-                    cols = slice((2 * pair + q) * P, (2 * pair + q + 1) * P)
-                    multiply(acc[:, q * C : (q + 1) * C], (codes[:, cols], scales[:, cols]), h_mx[first + q])
-                nc.scalar.copy(out=y_rows[c][:, first * C : (first + 2) * C], in_=acc[:])
+                    codes = place([P, count * P], U32, f"w2_codes{c}_{part}", *where)
+                if part == 2 and scale_place is not None:
+                    scales = place([P, count * P], U8, f"w2_scales{c}", *scale_place)
+                else:
+                    scales = held.tile([P, count * P], U8, name=f"scales{part}", align_bytes=64)
+                quantize(codes[:], scales[:], w2_rounded[c][part])
+                for pair in range(count // 2):
+                    acc = banks_y.tile([P, 2 * C], F32, name="acc_y")
+                    e = first + 2 * pair
+                    for q in range(2):
+                        cols = slice((2 * pair + q) * P, (2 * pair + q + 1) * P)
+                        multiply(acc[:, q * C : (q + 1) * C], (codes[:, cols], scales[:, cols]), h_mx[e + q])
+                    nc.scalar.copy(out=y_rows[c][:, e * C : (e + 2) * C], in_=acc[:])
 
         def gather_results(c):
             early = work.tile([P, 2, T], F32, name="early_products", align_bytes=64)
-            products[c] = [early[:, r, :] for r in range(1 if c == 0 else 2)]
-            for r in range(len(products[c]), R):
-                where = ((10, (2 * r - 1) * QUARTER // 2), (8, r * QUARTER), (12, (r - 2) * QUARTER))[c]
+            products[c] = [early[:, r, :] for r in range(2)]
+            for r in range(2, R):
+                third = ((10, QUARTER), (8, 2 * QUARTER), (1, 0))[c]
+                where = third if r == 2 else ((W2_ROOMS[3], 0), (W2_ROOMS[5], 0), (1, QUARTER))[c]
                 products[c].append(place([P, T], F32, f"late_products{c}_{r}", *where)[:])
             if c < CHUNKS - 1:
                 order = [(r, slice(0, T)) for r in range(R)]
@@ -329,10 +333,10 @@ def tile_moe_tk_glu_sigmoid_kernel(
             terms = products[c]
             result = work.tile([P, T], F32, name="result")
             add_turned(c, second, 2)
-            back = turn_back(c, second, (12, 2 * QUARTER))
+            back = turn_back(c, second, (1, 2 * QUARTER))
             nc.vector.tensor_tensor(terms[2][:, second], terms[2][:, second], back[:], ADD)
             add_turned(c, first, 3)
-            back = turn_back(c, first, (12, 3 * QUARTER))
+            back = turn_back(c, first, (1, 3 * QUARTER))
             for tokens, partial in ((first, back[:]), (second, terms[2][:, second])):
                 nc.vector.tensor_tensor(result[:, tokens], terms[3][:, tokens], partial, ADD)
                 nc.sync.dma_start(out=out[c * P : (c + 1) * P, tokens], in_=result[:, tokens])
@@ -344,8 +348,7 @@ def tile_moe_tk_glu_sigmoid_kernel(
         everything = slice(0, P)
         for e in range(E):
             round_w13("w1", e, [("scalar", everything)])
-            cut = W3_ON_VECTOR[e] + W3_ON_GPSIMD[e]
-            shares = [("vector", slice(0, W3_ON_VECTOR[e])), ("gpsimd", slice(W3_ON_VECTOR[e], cut)), ("scalar", slice(cut, P))]
+            shares = [("vector", slice(0, W3_ON_VECTOR[e])), ("scalar", slice(W3_ON_VECTOR[e], P))]
             round_w13("w3", e, [share for share in shares if share[1].stop > share[1].start])
             if e >= 2:
                 quantize_h(e - 2)
@@ -362,18 +365,17 @@ def tile_moe_tk_glu_sigmoid_kernel(
             if 1 <= e < LAST:
                 gather_tokens((e - 1) % 2, AHEAD + (e - 1) // 2, 1, e)
         quantize_h(LAST - 1)
+        round_first_half()
         gated_units(LAST)
         quantize_h(LAST)
 
         for c in range(CHUNKS):
-            for half in range(2):
-                round_w2(c, half)
-            for half in range(2):
-                second_layer(c, half)
+            round_w2(c)
+            second_layer(c)
             if c >= 1:
                 gather_results(c - 1)
                 add_turned(c - 1, slice(0, T), R)
         for c in range(CHUNKS - 1):
-            store_chunk(c, (6, c * QUARTER))
+            store_chunk(c, (3, c * QUARTER))
         gather_results(CHUNKS - 1)
         store_last_chunk()

@@ -49,7 +49,7 @@ def tile_moe_tk_glu_sigmoid_kernel(
         banks_y = ctx.enter_context(tc.psum_pool(name="banks_y", bufs=2))
 
         def place(shape, dtype, name, room, start=0):
-            return placed.tile(shape, dtype, name=name, offset=room * ROOM + start, align_bytes=64)
+            return placed.tile(shape, dtype, name=name, offset=room * ROOM + start, align_bytes=256)
 
         gate_cols = place([P, R, T // P], F32, "gate_cols", ROUNDED_ROOM)
         nc.scalar.dma_start(out=gate_cols[:], in_=gate[:, 0, :].rearrange("r (q c) -> q r c", q=P))
@@ -64,7 +64,7 @@ def tile_moe_tk_glu_sigmoid_kernel(
         token_halves = [slice(half * (T // 2), (half + 1) * (T // 2)) for half in range(2)]
         x_raw = []
         for half, tokens in enumerate(token_halves):
-            raw_half = held.tile([P, PACK, T // 2], F32, name="x_raw", tag=f"last_sig{half}", align_bytes=64)
+            raw_half = held.tile([P, PACK, T // 2], F32, name="x_raw", tag=f"last_sig{half}", align_bytes=256)
             nc.sync.dma_start(out=raw_half[:], in_=xT[:, tokens].rearrange("(p j) t -> p j t", j=PACK))
             x_raw.append(raw_half)
         offs_t = held.tile([P, S // LIST_ROWS], U16, name="offs_t")
@@ -323,7 +323,7 @@ def tile_moe_tk_glu_sigmoid_kernel(
 
         def store_chunk(c, tag):
             back = turn_back(c, slice(0, T), tag)
-            result = work.tile([P, T], F32, name="result")
+            result = work.tile([P, T], F32, name="result", align_bytes=256)
             nc.scalar.copy(out=result[:], in_=back[:])
             nc.sync.dma_start(out=out[c * P : (c + 1) * P, :], in_=result[:])
 
@@ -331,7 +331,7 @@ def tile_moe_tk_glu_sigmoid_kernel(
             c = CHUNKS - 1
             first, second = token_halves
             terms = products[c]
-            result = work.tile([P, T], F32, name="result")
+            result = work.tile([P, T], F32, name="result", align_bytes=256)
             add_turned(c, second, 2)
             back = turn_back(c, second, (1, 2 * QUARTER))
             nc.vector.tensor_tensor(terms[2][:, second], terms[2][:, second], back[:], ADD)

@@ -33,6 +33,9 @@ AHEAD = 5
 WINDOW = 1408
 ROUNDED_ROOM = ROOMS
 W3_ON_VECTOR = (0, 96, 96, 96, 96, 96, 96, 128)
+RUN = R * T // P
+GATE_STEP = N * T * R // P - RUN
+GATE_START = (R - 1) * T + T - RUN
 FIRST_HALF_ENGINE = ("scalar", "vector", "scalar")
 
 
@@ -51,8 +54,9 @@ def tile_moe_tk_glu_sigmoid_kernel(
         def place(shape, dtype, name, room, start=0):
             return placed.tile(shape, dtype, name=name, offset=room * ROOM + start, align_bytes=256)
 
-        gate_cols = place([P, R, T // P], F32, "gate_cols", ROUNDED_ROOM)
-        nc.scalar.dma_start(out=gate_cols[:], in_=gate[:, 0, :].rearrange("r (q c) -> q r c", q=P))
+        gate_cols = place([P, RUN], F32, "gate_cols", ROUNDED_ROOM)
+        runs = gate.rearrange("r n t -> (r n t)")[GATE_START : GATE_START + P * GATE_STEP].rearrange("(q s) -> q s", q=P)
+        nc.scalar.dma_start(out=gate_cols[:], in_=runs[:, 0:RUN])
         ident = held.tile([P, P], F32, name="ident")
         make_identity(nc, ident[:])
 
@@ -94,11 +98,7 @@ def tile_moe_tk_glu_sigmoid_kernel(
 
         for e in range(E - 2):
             load_expert(e)
-        pos_t = []
-        for r, pos in enumerate((pos1, pos2, pos3, pos4)):
-            list_tile = held.tile([P, T // LIST_ROWS], U16, name=f"pos_t{r}")
-            nc.sync.dma_start(list_tile[:], pos)
-            pos_t.append(list_tile)
+        pos_t = [held.tile([P, T // LIST_ROWS], U16, name=f"pos_t{r}") for r in range(R)]
 
         gates = held.tile([P, R, T], F32, name="gates")
         for r in range(R):
@@ -107,8 +107,12 @@ def tile_moe_tk_glu_sigmoid_kernel(
             else:
                 spread = banks_g.tile([P, T // P, P], F32, name="acc_w3")
             for c in range(T // P):
-                nc.tensor.transpose(spread[:, c, :], gate_cols[:, r, c : c + 1].to_broadcast([P, P]), ident[:])
-            nc.scalar.copy(out=gates[:, r, :].rearrange("p (q c) -> p q c", q=P), in_=spread[:].rearrange("p c q -> p q c"))
+                column = r * (T // P) + c
+                nc.tensor.transpose(spread[:, c, :], gate_cols[:, column : column + 1].to_broadcast([P, P]), ident[:])
+            nc.scalar.copy(
+                out=gates[:].rearrange("p r (a b c) -> p (r a) b c", b=R, c=T // P)[:, :, r, :].rearrange("p (r a) c -> p r a c", r=R),
+                in_=spread[:].rearrange("p c (r a) -> p r a c", r=R)[:, :, ::-1, :],
+            )
 
         def copy_on(engine, dst, src):
             if engine == "vector":
@@ -360,6 +364,9 @@ def tile_moe_tk_glu_sigmoid_kernel(
                 load_expert(LAST - 1 + e)
             elif e < LAST:
                 load_half((e - 2) // 2, e % 2)
+            if e == 1:
+                for list_tile, pos in zip(pos_t, (pos1, pos2, pos3, pos4)):
+                    nc.sync.dma_start(list_tile[:], pos)
             if e == LAST - 1:
                 load_half(CHUNKS - 1, 1)
             if 1 <= e < LAST:

@@ -277,7 +277,10 @@ def tile_moe_tk_glu_sigmoid_kernel(
                     scales = held.tile([P, count * P], U8, name=f"scales{part}", align_bytes=64)
                 quantize(codes[:], scales[:], w2_rounded[c][part])
                 for pair in range(count // 2):
-                    acc = banks_y.tile([P, 2 * C], F32, name="acc_y")
+                    if part == 0:
+                        acc = banks_y.tile([P, 2 * C], F32, name="acc_y")
+                    else:
+                        acc = banks_a.tile([P, 2 * C], F32, name="acc_w1")
                     e = first + 2 * pair
                     for q in range(2):
                         cols = slice((2 * pair + q) * P, (2 * pair + q + 1) * P)

@@ -206,7 +206,7 @@ def tile_moe_tk_glu_sigmoid_kernel(
                         (w_codes[:, cols], w_scales[:, cols]),
                         (slot_codes[:, slots], slot_scales[:, slots]),
                     )
-                sums[e, s, kind] = acc[:].rearrange("p t (c i) -> p c t i", i=2)
+                sums[e, s, kind] = acc[:].rearrange("p t s -> p s t")
 
         def gated_units(e):
             h = work.tile([P, C, PACK], BF16, name="h", align_bytes=64)
@@ -219,10 +219,10 @@ def tile_moe_tk_glu_sigmoid_kernel(
                     host = place([P, PACK * P], F32, f"sig{e}_{s}", room_of("w1", LAST), (2 + s) * QUARTER)
                 else:
                     host = place([P, PACK * P], F32, f"sig{e}_{s}", room_of("w1", e + 1), s * QUARTER)
-                sig = host[:].rearrange("p (c t i) -> p c t i", t=PACK, i=2)
+                sig = host[:].rearrange("p (s t) -> p s t", t=PACK)
                 nc.scalar.activation(sig, sums[e, s, "w1"], SIGMOID)
                 nc.vector.tensor_tensor(
-                    h[:, slots, :].rearrange("p (c i) t -> p c t i", i=2), sig, sums[e, s, "w3"], MULT
+                    h[:, slots, :], sig, sums[e, s, "w3"], MULT
                 )
 
         def quantize_h(e):

from contextlib import ExitStack

import concourse.mybir as mybir
from concourse.masks import make_identity

E, C, T, K, H, N, R = 8, 256, 512, 512, 512, 384, 4
S = E * C
FLOPS = 2 * S * (2 * K * H + H * N)
BYTES = 4 * (K * T + E * (2 * K * H + H * N) + R * T + N * T) + 2 * 128 * (S + R * T) // 16

F32 = mybir.dt.float32
BF16 = mybir.dt.bfloat16
U32 = mybir.dt.uint32
U16 = mybir.dt.uint16
U8 = mybir.dt.uint8
FP8X4 = mybir.dt.float8_e4m3fn_x4
SIGMOID = mybir.ActivationFunctionType.Sigmoid
MULT = mybir.AluOpType.mult
ADD = mybir.AluOpType.add

P = 128
PACK = 4
LIST_ROWS = 16
CHUNKS = N // P
HALF = E // 2
LAST = E - 1
WIDE = H * PACK
ROOM = 4 * PACK * H
ROOMS = 13
QUARTER = ROOM // 4
W2_ROOMS = (5, 7, 9, 11, 2, 6)
AHEAD = 5
WINDOW = 1408
ROUNDED_ROOM = ROOMS
W3_ON_VECTOR = (0, 96, 96, 96, 96, 96, 96, 128)
RUN = R * T // P
GATE_STEP = N * T * R // P - RUN
GATE_START = (R - 1) * T + T - RUN
FIRST_HALF_ENGINE = ("scalar", "vector", "scalar")


def tile_moe_tk_glu_sigmoid_kernel(
    tc, xT, w1, w3, w2, gate, offs, pos1, pos2, pos3, pos4, out
):
    nc = tc.nc
    with ExitStack() as ctx:
        held = ctx.enter_context(tc.tile_pool(name="held", bufs=1))
        placed = ctx.enter_context(tc.tile_pool(name="placed", bufs=1))
        work = ctx.enter_context(tc.tile_pool(name="work", bufs=2))
        banks_a = ctx.enter_context(tc.psum_pool(name="banks_a", bufs=3))
        banks_g = ctx.enter_context(tc.psum_pool(name="banks_g", bufs=3))
        banks_y = ctx.enter_context(tc.psum_pool(name="banks_y", bufs=2))

        def place(shape, dtype, name, room, start=0):
            return placed.tile(shape, dtype, name=name, offset=room * ROOM + start, align_bytes=256)

        gate_cols = place([P, RUN], F32, "gate_cols", ROUNDED_ROOM)
        runs = gate.rearrange("r n t -> (r n t)")[GATE_START : GATE_START + P * GATE_STEP].rearrange("(q s) -> q s", q=P)
        nc.scalar.dma_start(out=gate_cols[:], in_=runs[:, 0:RUN])
        ident = held.tile([P, P], F32, name="ident")
        make_identity(nc, ident[:])

        x_codes = held.tile([P, WINDOW], U32, name="x_codes", align_bytes=64)
        x_scales = held.tile([P, WINDOW], U8, name="x_scales", align_bytes=64)
        nc.gpsimd.memset(x_scales[:].bitcast(U32), 0)
        nc.gpsimd.memset(x_codes[:, T:], 0)

        token_halves = [slice(half * (T // 2), (half + 1) * (T // 2)) for half in range(2)]
        x_raw = []
        for half, tokens in enumerate(token_halves):
            raw_half = held.tile([P, PACK, T // 2], F32, name="x_raw", tag=f"last_sig{half}", align_bytes=256)
            nc.sync.dma_start(out=raw_half[:], in_=xT[:, tokens].rearrange("(p j) t -> p j t", j=PACK))
            x_raw.append(raw_half)
        offs_t = held.tile([P, S // LIST_ROWS], U16, name="offs_t")
        nc.sync.dma_start(offs_t[:], offs)

        raws = {}

        def room_of(kind, e):
            n = 2 * e + (kind == "w3")
            return n if n < ROOMS else {13: 0, 14: 1, 15: 3}[n]

        def load_expert(e):
            for kind, matrix in (("w1", w1), ("w3", w3)):
                raw = place([P, PACK, H], F32, f"{kind}_{e}", room_of(kind, e))
                nc.sync.dma_start(out=raw[:], in_=matrix[e, :, :].rearrange("(p j) h -> p j h", j=PACK))
                raws[kind, e] = raw

        def load_half(c, half):
            room = W2_ROOMS[2 * c + half]
            groups = ((0, 4),) if half == 0 else ((4, 2), (6, 2))
            for first, count in groups:
                raw = place([P, count, PACK, P], F32, f"w2_{c}_{first}", room, first % HALF * QUARTER)
                for q in range(count):
                    columns = w2[first + q, :, c * P : (c + 1) * P]
                    nc.sync.dma_start(out=raw[:, q], in_=columns.rearrange("(p j) n -> p j n", j=PACK))
                raws[c, first] = raw

        for e in range(E - 2):
            load_expert(e)
        pos_t = [held.tile([P, T // LIST_ROWS], U16, name=f"pos_t{r}") for r in range(R)]

        gates = held.tile([P, R, T], F32, name="gates")
        for r in range(R):
            if r % 2 == 0:
                spread = banks_a.tile([P, T // P, P], F32, name="acc_w1")
            else:
                spread = banks_g.tile([P, T // P, P], F32, name="acc_w3")
            for c in range(T // P):
                column = r * (T // P) + c
                nc.tensor.transpose(spread[:, c, :], gate_cols[:, column : column + 1].to_broadcast([P, P]), ident[:])
            nc.scalar.copy(
                out=gates[:].rearrange("p r (a b c) -> p (r a) b c", b=R, c=T // P)[:, :, r, :].rearrange("p (r a) c -> p r a c", r=R),
                in_=spread[:].rearrange("p c (r a) -> p r a c", r=R)[:, :, ::-1, :],
            )

        def copy_on(engine, dst, src):
            if engine == "vector":
                nc.vector.tensor_copy(out=dst, in_=src)
            else:
                nc.scalar.copy(out=dst, in_=src)

        def interleave(engine, dst, src):
            copy_on(
                engine,
                dst.rearrange("p (c i j) -> p c j i", i=PACK, j=PACK),
                src.rearrange("p j (c i) -> p c j i", i=PACK),
            )

        def quantize(codes, scales, values):
            nc.vector.quantize_mx(out=codes.bitcast(FP8X4), scales=scales, in_=values)

        def multiply(acc, stationary, moving):
            nc.tensor.matmul_mx(
                out=acc,
                lhsT=stationary[0].bitcast(FP8X4),
                lhsT_scale=stationary[1],
                rhs=moving[0].bitcast(FP8X4),
                rhs_scale=moving[1],
                start=True,
                stop=True,
            )

        x_rounded = held.tile([P, T * PACK], BF16, name="x_rounded", align_bytes=64)
        for half, tokens in enumerate(token_halves):
            values = x_rounded[:, tokens.start * PACK : tokens.stop * PACK]
            interleave("vector", values, x_raw[half][:])
            quantize(x_codes[:, tokens], x_scales[:, tokens], values)

        y_rows = [held.tile([P, S], F32, name=f"y_rows{c}") for c in range(CHUNKS)]
        slots_mx, w13_mx, sums, h_rounded, h_mx = {}, {}, {}, {}, {}
        w2_rounded, w2_mx, products, turned = {}, {}, {}, {}

        def gather_tokens(sort, first, count, step):
            entries = offs_t[:, first * (C // LIST_ROWS) : (first + count) * (C // LIST_ROWS)]
            window, dtype = ((x_codes, U32), (x_scales, U8))[sort]
            name = f"slots{sort}_{first}"
            if step == 0:
                picked = held.tile([P, count * C], dtype, name=name, align_bytes=64)
            else:
                picked = place([P, count * C], dtype, name, room_of("w1", step))
            nc.vector.tensor_copy(picked[:], window[:].indirect(entries))
            for q in range(count):
                slots_mx[sort, first + q] = picked[:, q * C : (q + 1) * C]

        w13_rounded = place([P, 3 * WIDE], BF16, "w13_rounded", ROUNDED_ROOM)

        def places(e):
            return {"w1": 2 * (e % 2), "w3": 1}

        def round_w13(kind, e, shares):
            src = raws[kind, e][:].rearrange("p j (m t) -> p m j t", t=PACK)
            dst = w13_rounded[:, places(e)[kind] * WIDE : (places(e)[kind] + 1) * WIDE].rearrange("p (t m j) -> p m j t", t=PACK, j=PACK)
            for engine, ms in shares:
                copy_on(engine, dst[:, ms], src[:, ms])

        def quantize_w13(e):
            if e < LAST:
                codes = work.tile([P, 2 * H], U32, name="w13_codes", align_bytes=64)
                scales = work.tile([P, 2 * H], U8, name="w13_scales", align_bytes=64)
                quantize(codes[:], scales[:], w13_rounded[:, e % 2 * WIDE : (e % 2 + 2) * WIDE])
                for kind in ("w1", "w3"):
                    k = places(e)[kind] - e % 2
                    w13_mx[kind, e] = (codes[:, k * H : (k + 1) * H], scales[:, k * H : (k + 1) * H])
                return
            for k, kind in enumerate(("w1", "w3")):
                codes = place([P, H], U32, f"last_codes_{kind}", room_of("w1", LAST) - 1 + k)
                scales = held.tile([P, H], U8, name=f"last_scales_{kind}", align_bytes=64)
                start = places(e)[kind] * WIDE
                quantize(codes[:], scales[:], w13_rounded[:, start : start + WIDE])
                w13_mx[kind, e] = (codes[:], scales[:])

        def first_products(e):
            slot_codes, slot_scales = slots_mx[0, e], slots_mx[1, e]
            order = [(s, kind) for s in range(C // P) for kind in ("w1", "w3")]
            if e == LAST:
                order = [(s, kind) for kind in ("w1", "w3") for s in range(C // P)]
            for s, kind in order:
                slots = slice(s * P, (s + 1) * P)
                w_codes, w_scales = w13_mx[kind, e]
                acc = (banks_a if kind == "w1" else banks_g).tile([P, PACK, P], F32, name=f"acc_{kind}")
                for t in range(PACK):
                    cols = slice(t * P, (t + 1) * P)
                    multiply(
                        acc[:, t, :],
                        (w_codes[:, cols], w_scales[:, cols]),
                        (slot_codes[:, slots], slot_scales[:, slots]),
                    )
                sums[e, s, kind] = acc[:].rearrange("p t s -> p s t")

        def gated_units(e):
            h = work.tile([P, C, PACK], BF16, name="h", align_bytes=64)
            h_rounded[e] = h
            for s in range(C // P):
                slots = slice(s * P, (s + 1) * P)
                if e == LAST:
                    host = place([P, PACK * P], F32, f"sig{e}_{s}", W2_ROOMS[0], s * QUARTER)
                elif e == LAST - 1:
                    host = place([P, PACK * P], F32, f"sig{e}_{s}", room_of("w1", LAST), (2 + s) * QUARTER)
                else:
                    host = place([P, PACK * P], F32, f"sig{e}_{s}", room_of("w1", e + 1), s * QUARTER)
                sig = host[:].rearrange("p (s t) -> p s t", t=PACK)
                nc.scalar.activation(sig, sums[e, s, "w1"], SIGMOID)
                nc.vector.tensor_tensor(
                    h[:, slots, :], sig, sums[e, s, "w3"], MULT
                )

        def quantize_h(e):
            codes = held.tile([P, C], U32, name=f"h_codes{e}", align_bytes=64)
            scales = held.tile([P, C], U8, name=f"h_scales{e}", align_bytes=64)
            quantize(codes[:], scales[:], h_rounded[e][:].rearrange("p s t -> p (s t)"))
            h_mx[e] = (codes[:], scales[:])

        def round_pieces(engine, dst, src):
            copy_on(
                engine,
                dst.rearrange("p (q c i j) -> p q c j i", c=P // PACK, i=PACK, j=PACK),
                src.rearrange("p q j (c i) -> p q c j i", i=PACK),
            )

        def round_first_half():
            for part in range(2):
                values = w13_rounded[:, part * WIDE // 2 : (part + 1) * WIDE // 2]
                round_pieces("scalar", values, raws[0, 0][:, 2 * part : 2 * part + 2])

        def round_w2(c):
            width = 2 * P * PACK
            room = W2_ROOMS[2 * c + 1]
            if c == 0:
                pairs = [w13_rounded[:, start : start + width] for start in (0, width, 2 * WIDE)]
                w2_rounded[c] = [w13_rounded[:, 0:WIDE], pairs[2]]
            else:
                values = place([P, WIDE], BF16, f"w2_rounded{c}", *((W2_ROOMS[0], 0), (8, 0))[c - 1])
                third = place([P, width], BF16, f"w2_third{c}", *((10, QUARTER), (8, 2 * QUARTER))[c - 1])
                pairs = [values[:, 0:width], values[:, width:WIDE], third[:]]
                w2_rounded[c] = [values[:], third[:]]
            for part in range(2 if c > 0 else 0):
                round_pieces(FIRST_HALF_ENGINE[c], pairs[part], raws[c, 0][:, 2 * part : 2 * part + 2])
            round_pieces("scalar", pairs[2], raws[c, 4][:])
            last = place([P, width], BF16, f"w2_last{c}", room)
            round_pieces("vector", last[:], raws[c, 6][:])
            w2_rounded[c].append(last[:])

        def second_layer(c):
            first_place = (None, (8, QUARTER // 2), (12, 0))[c]
            last_place = ((10, QUARTER), (12, 0), (3, QUARTER - P * 4))[c]
            scale_place = (None, (8, 2 * QUARTER), None)[c]
            for part, (first, count) in enumerate(((0, 4), (4, 2), (6, 2))):
                where = (first_place, None, last_place)[part]
                if where is None:
                    codes = held.tile([P, count * P], U32, name=f"codes{part}", align_bytes=64)
                else:
                    codes = place([P, count * P], U32, f"w2_codes{c}_{part}", *where)
                if part == 2 and scale_place is not None:
                    scales = place([P, count * P], U8, f"w2_scales{c}", *scale_place)
                else:
                    scales = held.tile([P, count * P], U8, name=f"scales{part}", align_bytes=64)
                quantize(codes[:], scales[:], w2_rounded[c][part])
                for pair in range(count // 2):
                    if part == 0:
                        acc = banks_y.tile([P, 2 * C], F32, name="acc_y")
                    else:
                        acc = banks_a.tile([P, 2 * C], F32, name="acc_w1")
                    e = first + 2 * pair
                    for q in range(2):
                        cols = slice((2 * pair + q) * P, (2 * pair + q + 1) * P)
                        multiply(acc[:, q * C : (q + 1) * C], (codes[:, cols], scales[:, cols]), h_mx[e + q])
                    nc.scalar.copy(out=y_rows[c][:, e * C : (e + 2) * C], in_=acc[:])

        def gather_results(c):
            early = work.tile([P, 2, T], F32, name="early_products", align_bytes=64)
            products[c] = [early[:, r, :] for r in range(2)]
            for r in range(2, R):
                third = ((10, QUARTER), (8, 2 * QUARTER), (1, 0))[c]
                where = third if r == 2 else ((W2_ROOMS[3], 0), (W2_ROOMS[5], 0), (1, QUARTER))[c]
                products[c].append(place([P, T], F32, f"late_products{c}_{r}", *where)[:])
            if c < CHUNKS - 1:
                order = [(r, slice(0, T)) for r in range(R)]
            else:
                first, second = token_halves
                order = [(0, second), (1, second), (0, first), (1, first), (2, first), (2, second), (3, first), (3, second)]
            for r, tokens in order:
                entries = pos_t[r][:, tokens.start // LIST_ROWS : tokens.stop // LIST_ROWS]
                nc.vector.tensor_tensor(products[c][r][:, tokens], y_rows[c][:].indirect(entries), gates[:, r, tokens], MULT)

        def blocks(tokens):
            return [slice(b, b + P) for b in range(0, tokens.stop - tokens.start, P)]

        def add_turned(c, tokens, count):
            acc = banks_g.tile([P, tokens.stop - tokens.start], F32, name="acc_w3")
            for r in range(count):
                for cols in blocks(tokens):
                    nc.tensor.matmul(
                        acc[:, cols],
                        lhsT=products[c][r][:, tokens][:, cols],
                        rhs=ident[:],
                        start=r == 0 and cols.start == 0,
                        stop=r == count - 1 and cols.stop == tokens.stop - tokens.start,
                        is_transpose=True,
                    )
            turned[c, tokens.start] = acc

        def turn_back(c, tokens, tag):
            staged = place([P, tokens.stop - tokens.start], F32, f"staged{c}_{tokens.start}", *tag)
            nc.scalar.copy(out=staged[:], in_=turned[c, tokens.start][:])
            back = banks_a.tile([P, tokens.stop - tokens.start], F32, name="acc_w1")
            for cols in blocks(tokens):
                nc.tensor.transpose(back[:, cols], staged[:, cols], ident[:])
            return back

        def store_chunk(c, tag):
            back = turn_back(c, slice(0, T), tag)
            result = work.tile([P, T], F32, name="result", align_bytes=256)
            nc.scalar.copy(out=result[:], in_=back[:])
            nc.sync.dma_start(out=out[c * P : (c + 1) * P, :], in_=result[:])

        def store_last_chunk():
            c = CHUNKS - 1
            first, second = token_halves
            terms = products[c]
            result = work.tile([P, T], F32, name="result", align_bytes=256)
            add_turned(c, second, 2)
            back = turn_back(c, second, (1, 2 * QUARTER))
            nc.vector.tensor_tensor(terms[2][:, second], terms[2][:, second], back[:], ADD)
            add_turned(c, first, 3)
            back = turn_back(c, first, (1, 3 * QUARTER))
            for tokens, partial in ((first, back[:]), (second, terms[2][:, second])):
                nc.vector.tensor_tensor(result[:, tokens], terms[3][:, tokens], partial, ADD)
                nc.sync.dma_start(out=out[c * P : (c + 1) * P, tokens], in_=result[:, tokens])

        for first, count in ((0, HALF), (HALF, AHEAD - HALF)):
            for sort in range(2):
                gather_tokens(sort, first, count, 0)

        everything = slice(0, P)
        for e in range(E):
            round_w13("w1", e, [("scalar", everything)])
            shares = [("vector", slice(0, W3_ON_VECTOR[e])), ("scalar", slice(W3_ON_VECTOR[e], P))]
            round_w13("w3", e, [share for share in shares if share[1].stop > share[1].start])
            if e >= 2:
                quantize_h(e - 2)
            quantize_w13(e)
            if e >= 1:
                gated_units(e - 1)
            first_products(e)
            if e < 2:
                load_expert(LAST - 1 + e)
            elif e < LAST:
                load_half((e - 2) // 2, e % 2)
            if e == 1:
                for list_tile, pos in zip(pos_t, (pos1, pos2, pos3, pos4)):
                    nc.sync.dma_start(list_tile[:], pos)
            if e == LAST - 1:
                load_half(CHUNKS - 1, 1)
            if 1 <= e < LAST:
                gather_tokens((e - 1) % 2, AHEAD + (e - 1) // 2, 1, e)
        quantize_h(LAST - 1)
        round_first_half()
        gated_units(LAST)
        quantize_h(LAST)

        for c in range(CHUNKS):
            round_w2(c)
            second_layer(c)
            if c >= 1:
                gather_results(c - 1)
                add_turned(c - 1, slice(0, T), R)
        for c in range(CHUNKS - 1):
            store_chunk(c, (3, c * QUARTER))
        gather_results(CHUNKS - 1)
        store_last_chunk()
